import numpy as np, ml_dtypes
CORES = [3,7,11,15,131,135,139,143]
N = 8
BF = ml_dtypes.bfloat16
def gentries(a):
    return np.ascontiguousarray(a.reshape(8, 16, -1).transpose(0, 2, 1)).reshape(8, -1)
def gtable(e):
    e = np.asarray(e); return np.ascontiguousarray(e.reshape(8, -1, 16).transpose(0, 2, 1)).reshape(128, -1).astype(np.int32)
W, K, RO, S, TH, AG = 1664, 256, 2, 5, 66, 9
L0 = 16 - RO
B = K // N
def hubbed(rng, hub, n, share):
    return np.where(rng.random((N, 8, n)) < share, np.take_along_axis(hub, rng.integers(0, 32, (N, 8, n)), 2), rng.integers(0, W, (N, 8, n)))
def parts(rng):
    x = np.where(rng.random((N, 8, 1, W)) < 0.875, rng.integers(0, 16, (N, 8, 16, W)), rng.integers(4, 12, (N, 8, 16, W)))
    hub = rng.integers(0, W, (N, 8, 32)); a = hubbed(rng, hub, L0 * W, 0.1).reshape(N, 8, L0, W)
    a = np.where(rng.random(a.shape) < rng.choice(np.array([0.05, 0.2, 0.45]), (N, 8, 1, 1)), -1, a)
    return x, a, hubbed(rng, hub, W, 0.25), rng.integers(0, W, (N, 8, K))
def pack(x, a, s, p):
    a = np.concatenate([a, np.full((N, 8, RO, W), -1)], axis=2)
    return {"x0": np.ascontiguousarray(x.reshape(N, 128, W)).astype(np.float32).astype(BF), "lk": np.ascontiguousarray(a.reshape(N, 128, W)).astype(np.int32),
            "nx": np.ascontiguousarray(s).astype(np.int32), "w0": np.stack([gtable(e) for e in p])}
def setup_inputs(rng):
    return pack(*parts(rng))
def setup_inputs_ties(rng):
    x, a, s, p = parts(rng); h = W // 2
    x[..., :h] = rng.integers(0, 16, (N, 8, 16, h))
    t = TH - 1 + rng.integers(0, 3, (N, 8, 1, h)); o = np.argsort(rng.random((N, 8, 16, h)), axis=2)
    x[..., h:2 * h] = x[..., :h] + np.where(x[..., :h] < 8, 1, -1) * ((t >> 4) + (o < (t & 15)))
    i = np.arange(L0)[None, None, :, None]; at = rng.integers(0, L0, (N, 8, 1, h)); bare = rng.random((N, 8, 1, h)) < 0.5
    a[..., :h] = np.where(i == at, h + np.arange(h), np.where((i > at) | bare, -1, a[..., :h]))
    return pack(x, a, s, rng.integers(0, h, (N, 8, K)))
def setup_inputs_votes(rng):
    x, a, s, p = parts(rng); h = K // 2
    for q in range(N):
        for g in range(8):
            if q < N - 1 and g % 4 == 3: continue
            c = rng.permutation(W)[:K * (S + 1)].reshape(K, S + 1); a[q, g] = -1
            s[q, g, c[:, :S]] = c[:, 1:]
            if q == N - 1:
                y = rng.integers(5, 8, (16, K, S)); e = np.where(np.arange(K) < h, 15, rng.integers(8, 11, (16, K)))
                s[q, g, c[:h, S]] = c[h + rng.permutation(h), 2]
                p[q, g] = c[:, 0]
            elif g % 2 == 1:
                n = K - 1 if g == 1 else int(rng.integers(h, K))
                y = rng.integers(0, 8, (16, K, S)); y[rng.permutation(16)[AG - 1:], n] += 8
                e = rng.integers(0, 16, (16, K)); e[:, 0] = 8
                s[q, g, c[:, S - 1]] = c[0, S]
                p[q, g] = c[:, 0]
            else:
                y = rng.integers(2, 14, (16, K, S)); y[:, h:] = np.where(rng.random((1, K - h, 1)) < 0.5, 2, 13)
                z = y[:, :, 0]
                for k in range(1, S): z = (z + y[:, :, k]) >> 1
                o = np.argsort(rng.random((16, K)), axis=0); n = AG - 1 + rng.integers(0, 3, (1, K))
                e = z + np.where(o < n, rng.integers(1, 3, (16, K)), -rng.integers(0, 2, (16, K)))
                s[q, g, c[h:, S - 1]] = np.where(rng.random(K - h) < 0.75, c[:K - h, S], c[h:, S])
                p[q, g] = c[rng.permutation(K), 0]
            x[q, g][:, c[:, :S].reshape(-1)] = y.reshape(16, K * S); x[q, g][:, c[:, S]] = e
    return pack(x, a, s, p)
def setup_inputs_alike(rng):
    x, a, s, p = parts(rng); few = np.array([0, W - 1, W // 2, 5])
    a[:, ::2] = np.where(a[:, ::2] < 0, -1, rng.choice(few, (N, 4, L0, W)))
    a[:, 1] = np.where(a[:, 1] < 0, -1, np.arange(W)); s[:, 1] = np.arange(W)
    s[:, 0] = W - 1; s[:, 4] = 0; s[:, 2] = rng.choice(few, (N, W))
    p[:, 3] = p[:, 3, :1]; p[:, 5] = rng.choice(few, (N, K)); p[:, 6] = np.where(rng.random((N, K)) < 0.5, 0, W - 1)
    return pack(x, a, s, p)
def setup_inputs_full(rng):
    x, a, s, p = parts(rng)
    x[:, ::2] = rng.integers(6, 10, (N, 4, 16, W)); x[:, 1::2] = 15 * rng.integers(0, 2, (N, 4, 16, W))
    a = np.where(a < 0, rng.integers(0, W, a.shape), a)
    return pack(x, a, s, p)
def setup_inputs_spread(rng):
    x, a, s, p = parts(rng)
    x = np.minimum((np.exp2(1 + 3 * rng.random((N, 8, 1, W))) * rng.random((N, 8, 16, W))).astype(np.int64), 15)
    a = np.where(a < 0, -1, (W * rng.random(a.shape) ** 3).astype(np.int64)); s = (W * rng.random(s.shape) ** 2).astype(np.int64)
    return pack(x, np.minimum(a, W - 1), np.minimum(s, W - 1), p)
def check_inputs(d):
    bad = []
    x = d["x0"].astype(np.float32)
    if not np.all((x >= 0) & (x <= 15) & (x == np.floor(x))): bad.append("x0 whole numbers from 0 to 15")
    for k, lo in (("lk", -1), ("nx", 0), ("w0", 0)):
        if np.min(d[k]) < lo or np.max(d[k]) > W - 1: bad.append("range of " + k)
    if np.any(d["lk"].reshape(-1, 8, 16, W)[:, :, L0:] != -1): bad.append("upper links of lk empty")
    return bad
def reference(x0, lk, nx, w0):
    M = W + RO * K
    X = np.zeros((N, 8, 16, M), np.int64); X[..., :W] = x0.astype(np.float32).astype(np.int64).reshape(N, 8, 16, W)
    ad = np.full((N, 8, 16, M), -1, np.int64); ad[..., :W] = lk.reshape(N, 8, 16, W)
    sc = np.zeros((N, 8, M), np.int64); sc[..., :W] = nx
    v = np.stack([gentries(e) for e in w0]).astype(np.int64)
    i = np.arange(16)[:, None]
    for t in range(RO):
        n = W + t * K; Z = np.zeros((N, 8, 16, K), np.int64)
        for r in range(N):
            for g in range(8):
                x, a, s, p = X[r, g], ad[r, g], sc[r, g], v[r, g]
                z = x[:, p]; l = np.full(K, 16)
                for k in range(S):
                    c = a[:, p]
                    dist = np.add.reduce(np.abs(x[:, np.maximum(c, 0)] - z[:, None, :]), axis=0)
                    b = np.max(np.where((c >= 0) & (dist < TH) & (i < l), i, -1), axis=0)
                    p = np.where(b >= 0, c[np.maximum(b, 0), np.arange(K)], s[p]); l = np.where(b >= 0, b, l)
                    y = x[:, p]; yes = np.add.reduce((y > z).astype(np.int64), axis=0) >= AG
                    z = (z + y) >> 1
                Z[r, g] = z; v[r, g] = p
                ends = np.zeros(M, bool); ends[p] = True
                no = np.zeros(M, bool); no[p[~yes]] = True
                x[::2] = np.where(ends & ~no, 15 - x[::2], x[::2])
                u, first = np.unique(p, return_index=True)
                a[L0 + t, u] = n + first; s[n:n + K] = s[p]
        for r in range(N):
            for q in range(N):
                X[q, :, :, n + r * B:n + (r + 1) * B] = np.roll(Z[r, :, :, q * B:(q + 1) * B], (q - r) % N, axis=0)
    return {"yx": X.reshape(N, 128, M).astype(np.float32).astype(BF), "yv": v.astype(np.float32)}

@@ -1,0 +1,542 @@
+import numpy as np
+from concourse.bass import DstId, RemoteDMATransfer
+from concourse.mybir import dt, AluOpType as Op, AxisListType, ActivationFunctionType as AF
+
+W, K, RO, S = 1664, 256, 2, 5
+GB = 256
+N0 = GB + 8
+XC = N0 + W + RO * K
+AC = N0 + W + K
+MAGIC = 12582912.0
+KZ = 4
+
+SCRATCH = {}
+
+
+def declare(where, dtype, names, shape):
+    for nm in names.split():
+        SCRATCH[nm] = (where, shape, dtype)
+
+
+declare("sbuf", "bfloat16", "X", [128, XC])
+declare("sbuf", "int32", "A", [128, AC])
+declare("sbuf", "int32", "w0s KI", [128, 16])
+declare("sbuf", "uint16", "VO OFX OFA", [128, 16])
+declare("sbuf", "bfloat16", "Y GT FY RB LE LO ZS0 ZS1 ZERO WR", [128, 256])
+declare("sbuf", "bfloat16", "junk", [128, 1024])
+declare("sbuf", "float32", "VAL YV AD cF", [128, 256])
+declare("sbuf", "float32", "ACV DV FF FR M16 M5 MN TR", [128, 16])
+declare("sbuf", "float32", "ACS", [128, 32])
+declare("sbuf", "float32", "KF", [128, 40])
+declare("sbuf", "bfloat16", "LAA LAB LBB IB IP IN ZM MK DC WC T2 Z0 Z1 NV0 NV1", [128, 128])
+declare("sbuf", "float16", "IH TRI PERM BLK WB WH AH0 AH1 LT0 LT1 HH0 HH1", [128, 128])
+declare("sbuf", "float32", "tF SAME PW", [128, 128])
+declare("sbuf", "int32", "cmI cgI", [128, 128])
+declare("sbuf", "int32", "cI", [128, 256])
+declare("sbuf", "int32", "pI", [128, 1])
+declare("sbuf", "bfloat16", "B2 BN B1 B4", [128, 8])
+declare("sbuf", "float16", "BH", [128, 8])
+declare("sbuf", "float16", "CT", [128, 256])
+declare("sbuf", "bfloat16", "D0 D1 M0 M1", [128, 2048])
+declare("sbuf", "uint16", "AO0 AO1", [128, 128])
+declare("sbuf", "bfloat16", "NT0 NT1", [128, 136])
+declare("sbuf", "float16", "SA0 SA1", [128, S * 128])
+declare("psum", "float32", "eA eB dist0 dist1 ch0 ch1 zp0 zp1", [128, 512])
+SEMAPHORES = ["qV", "qP", "qS", "qG", "ldw", "ldx", "ldal", "ldas", "ldn", "arr0", "arr1", "snt", "out1", "out2", "out3"]
+
+
+def rank_program(g, core, T, topo):
+    rank = T.rank_of(core)
+    if rank is None:
+        return
+    sem = T.sem
+    eng = {"V": g.vector, "P": g.tensor, "S": g.scalar, "G": g, "Y": g.sync}
+    qsem = {"V": "qV", "P": "qP", "S": "qS", "G": "qG"}
+    clock = {q: {} for q in eng}
+    cnt = {q: 0 for q in eng}
+    snap = {}
+    lastw, readers = {}, {}
+
+    def need(q, tok):
+        s, n = tok
+        if clock[q].get(s, 0) >= n:
+            return
+        eng[q].wait_ge(sem[s], n)
+        c = clock[q]
+        for k2, v2 in snap.get(tok, {}).items():
+            if c.get(k2, 0) < v2:
+                c[k2] = v2
+        c[s] = n
+
+    def deps(q, reads, writes, acc=()):
+        own = qsem.get(q)
+        want = {}
+        for k in reads:
+            for t in lastw.get(k, ()):
+                want[t[0]] = max(want.get(t[0], 0), t[1])
+        for k in list(writes) + list(acc):
+            for t in list(lastw.get(k, ())) + list(readers.get(k, ())):
+                if t[0] != own or (k not in acc and t in lastw.get(k, ())):
+                    want[t[0]] = max(want.get(t[0], 0), t[1])
+        for s, n in want.items():
+            need(q, (s, n))
+
+    def op(q, f, reads, writes, acc=()):
+        deps(q, reads, writes, acc)
+        f().then_inc(sem[qsem[q]], 1)
+        cnt[q] += 1
+        tok = (qsem[q], cnt[q])
+        snap[tok] = dict(clock[q])
+        for k in list(writes) + list(acc):
+            lastw[k] = [tok]
+            readers[k] = []
+        for k in reads:
+            readers.setdefault(k, []).append(tok)
+
+    def load(f, name, total, k):
+        f().then_inc(sem[name], 16)
+        lastw[k] = [t for t in lastw.get(k, []) if t[0] != name] + [(name, total)]
+
+    v, pe, act = g.vector, g.tensor, g.scalar
+
+    def ts(out, in0, s1, s2, o0, o1, reads, writes):
+        if o1 is None:
+            op("V", lambda: v.tensor_scalar(out, in0, s1, None, o0), reads, writes)
+        else:
+            op("V", lambda: v.tensor_scalar(out, in0, s1, s2, o0, o1), reads, writes)
+
+    def tt(out, a, b, o, reads, writes):
+        op("V", lambda: v.tensor_tensor(out, a, b, o), reads, writes)
+
+    def cp(out, in_, reads, writes):
+        op("V", lambda: v.tensor_copy(out, in_), reads, writes)
+
+    def ac(out, in_, f, reads, writes, **kw):
+        op("S", lambda: act.activation(out, in_, f, **kw), reads, writes)
+
+    def lin(out, in_, scale, bias, reads, k):
+        ac(out, in_, AF.Copy if isinstance(bias, float) else AF.Identity, reads, [k], scale=scale, bias=bias)
+
+    def mm(out, l, r, start, stop, reads, key):
+        op("P", lambda: pe.matmul(out, l, r, start, stop), reads, (), (key,))
+
+    load(lambda: g.sync.dma_start(T.w0s[:], T.w0[:]), "ldw", 16, "w0s")
+    for gg in range(4):
+        load(lambda: g.sync.dma_start(T.A[16 * gg:16 * gg + 15, N0:N0 + W], T.lk[16 * gg:16 * gg + 15, :]), "ldal", 64, "A")
+    for gg in range(4, 8):
+        load(lambda: act.dma_start(T.A[16 * gg:16 * gg + 15, N0:N0 + W], T.lk[16 * gg:16 * gg + 15, :]), "ldas", 64, "A")
+    load(lambda: g.sync.dma_start(T.A[15::16, N0:N0 + W], T.nx[:]), "ldn", 16, "A")
+    load(lambda: act.dma_start(T.X[:, N0:N0 + W], T.x0[:]), "ldx", 16, "X")
+
+    op("G", lambda: g.iota(T.pI[:], [[0, 1]], 0, 1), [], ["pI"])
+    op("G", lambda: g.iota(T.cI[:], [[1, 256]], 0, 0), [], ["cI"])
+    op("V", lambda: v.memset(T.ZERO[:], 0.0), [], ["ZERO"])
+
+    def stripe(nm, n, cmp, fill, base, step, cm, again=False):
+        op("G", lambda: g.affine_select(T[nm][:], T[nm][:] if again else T.ZERO[:, 0:n], [[step, n]], cmp, fill, base, cm), [nm] if again else ["ZERO"], [nm])
+    stripe("IB", 128, Op.not_equal, 1.0, 0, -1, 1)
+    stripe("IP", 128, Op.not_equal, 2048.0, 0, -1, 1)
+    stripe("IN", 128, Op.not_equal, -2048.0, 0, -1, 1)
+    stripe("WR", 256, Op.not_equal, 63.0 / 128, 0, -1, 1)
+    stripe("WR", 256, Op.not_equal, 63.0 / 128, 128, -1, 1, True)
+    stripe("T2", 128, Op.is_ge, 512.0, 0, 1, -1)
+    op("G", lambda: g.iota(T.cF[:], [[1, 256]], W, 0, allow_small_or_imprecise_dtypes=True), [], ["cF"])
+    op("V", lambda: v.memset(T.X[:, GB:N0], 127.0), [], ["Xd"])
+    op("V", lambda: v.memset(T.A[:, GB:N0], -1), [], ["Ad"])
+    op("V", lambda: v.memset(T.NT0[:, 0:1], 1.0), [], ["NTi0"])
+    op("V", lambda: v.memset(T.NT1[:, 0:1], 1.0), [], ["NTi1"])
+    op("V", lambda: v.memset(T.PW[:], 0.0), [], ["PW"])
+
+    def ci(j): return T.KI[:, j:j + 1]
+    def cf(j): return T.KF[:, j:j + 1]
+    def kk(j): return "KF%d" % j
+    def m16(j): return T.M16[:, j:j + 1]
+    ts(ci(0), T.pI[:], 15, None, Op.bitwise_and, None, ["pI"], ["KI0"])
+    ts(ci(1), T.pI[:], 4, None, Op.arith_shift_right, None, ["pI"], ["KI1"])
+    ts(ci(4), T.pI[:], 1, None, Op.bitwise_and, None, ["pI"], ["KI4"])
+    cp(cf(0), T.pI[:], ["pI"], [kk(0)])
+    cp(cf(1), ci(0), ["KI0"], [kk(1)])
+    cp(cf(2), ci(1), ["KI1"], [kk(2)])
+    ts(ci(5), ci(1), 1, None, Op.bitwise_and, None, ["KI1"], ["KI5"])
+    ts(T.cmI[:], T.cI[:, 0:128], 15, None, Op.bitwise_and, None, ["cI"], ["cmI"])
+    ts(T.cgI[:], T.cI[:, 0:128], 4, None, Op.arith_shift_right, None, ["cI"], ["cgI"])
+    P0, PM, PG = cf(0), cf(1), cf(2)
+    c128 = T.cI[:, 0:128]
+    ts(T.M16[:], T.cI[:, 0:16], PM, None, Op.is_equal, None, ["cI", kk(1)], ["M16"])
+    ts(cf(14), PM, 10.5, -1.5 + 2.0 ** -12, Op.is_lt, Op.mult, [kk(1)], [kk(14)])
+    ts(T.tF[:], T.cmI[:], 14.5, -1.0, Op.is_lt, Op.mult, ["cmI"], ["tF"])
+    ts(T.SAME[:], T.cgI[:], PG, None, Op.is_equal, None, ["cgI", kk(2)], ["SAME"])
+    for nm, f in (("B2", 2.0), ("BN", -1.0), ("B1", 1.0), ("BH", 1.0), ("B4", -4096.0)):
+        ts(T[nm][:], T.cI[:, 0:8], PG, f, Op.is_equal, Op.mult, ["cI", kk(2)], [nm])
+    tt(T.ZM[:], T.tF[:], T.SAME[:], Op.mult, ["tF", "SAME"], ["ZM"])
+    ts(T.DC[:], T.cmI[:], 15, None, Op.is_equal, None, ["cmI"], ["DC"])
+    lin(cf(6), PM, 1.0, -256.0, [kk(1)], kk(6))
+    lin(cf(15), m16(11), 7.5, 1.0, ["M16"], kk(15))
+    lin(cf(13), m16(13), -1.0, 0.0, ["M16"], kk(13))
+    lin(cf(16), m16(13), 126.5, cf(15), ["M16", kk(15)], kk(16))
+    lin(cf(18), cf(16), 1.0, cf(14), [kk(16), kk(14)], kk(18))
+    lin(cf(11), m16(15), 1.0, -1.0, ["M16"], kk(11))
+    lin(cf(12), m16(14), 1.0, -1.0, ["M16"], kk(12))
+    lin(cf(29), m16(12), -11264.0, m16(11), ["M16"], kk(29))
+    lin(cf(28), m16(13), 1.0, m16(15), ["M16"], kk(28))
+    lin(cf(31), cf(29), 1.0, m16(14), ["M16", kk(29)], kk(31))
+    lin(cf(32), cf(28), 512.0, cf(31), [kk(28), kk(31)], kk(32))
+    lin(T.M5[:], T.M16[:], 512.0, 0.0, ["M16"], "M5")
+    lin(T.MN[:], T.M16[:], 1e6, -1e6, ["M16"], "MN")
+    lin(T.AD[:], T.cF[:], m16(14), cf(12), ["cF", "M16", kk(12)], "AD")
+    ts(ci(2), ci(0), -1, 30, Op.mult, Op.add, ["KI0"], ["KI2"])
+    tt(cf(3), P0, PM, Op.subtract, [kk(0), kk(1)], [kk(3)])
+    ts(ci(3), ci(2), 15, None, Op.bitwise_and, None, ["KI2"], ["KI3"])
+    ts(cf(4), PM, 14.5, -2048.0, Op.is_lt, Op.mult, [kk(1)], [kk(4)])
+    tt(cf(5), ci(3), cf(3), Op.add, ["KI3", kk(3)], [kk(5)])
+    ts(T.BLK[:], T.cgI[:], PG, None, Op.is_equal, None, ["cgI", kk(2)], ["BLK"])
+    ts(T.PERM[:], c128, cf(5), None, Op.is_equal, None, ["cI", kk(5)], ["PERM"])
+    ts(T.MK[:], T.cmI[:], PM, None, Op.is_equal, None, ["cmI", kk(1)], ["MK"])
+    ts(cf(7), m16(15), -1000.0, P0, Op.mult, Op.add, ["M16", kk(0)], [kk(7)])
+    ts(T.tF[:], c128, cf(7), 1024.0, Op.is_le, Op.mult, ["cI", kk(7)], ["tF"])
+    tt(T.TRI[:], T.tF[:], T.SAME[:], Op.mult, ["tF", "SAME"], ["TRI"])
+    ts(T.VO[:], T.w0s[:], 8, None, Op.add, None, ["w0s"], ["VO0", "VO1"])
+    deferred = []
+
+    def later(f, *a):
+        deferred.append(lambda: f(*a))
+    later(cp, T.IH[:], T.IB[:], ["IB"], ["IH"])
+    later(ts, cf(8), ci(4), 2.0, -1.0, Op.mult, Op.add, ["KI4"], [kk(8)])
+    later(ts, cf(9), ci(4), -15.0, 15.0, Op.mult, Op.add, ["KI4"], [kk(9)])
+    later(ts, T.TR[:], T.cI[:, 0:16], 16, cf(6), Op.mult, Op.add, ["cI", kk(6)], ["TR"])
+    later(ts, cf(19), PM, 10.5, -1.0, Op.is_lt, Op.mult, [kk(1)], [kk(19)])
+    for j in range(11):
+        later(op, "V", lambda j=j: v.memset(T.PW[:, j::16], 2.0 ** -(j + 1)), ["PW"], ["PWx%d" % j])
+    later(tt, T.WB[:], T.PW[:], T.SAME[:], Op.mult, ["PW", "SAME"] + ["PWx%d" % j for j in range(11)], ["WB"])
+    later(ts, T.CT[:], T.cI[:], cf(13), cf(18), Op.mult, Op.add, ["cI", kk(13), kk(18)], ["CT"])
+    later(ts, T.WH[:], T.IB[:], cf(19), None, Op.mult, None, ["IB", kk(19)], ["WH"])
+    later(ts, T.tF[:], T.cmI[:], 11, -1.0, Op.is_equal, Op.mult, ["cmI"], ["tF"])
+    later(ts, cf(30), PM, 10.5, 2048.0, Op.is_lt, Op.mult, [kk(1)], [kk(30)])
+    later(cp, cf(26), ci(5), ["KI5"], [kk(26)])
+    later(ts, cf(27), ci(5), -1.0, 1.0, Op.mult, Op.add, ["KI5"], [kk(27)])
+    later(tt, T.WC[:], T.tF[:], T.SAME[:], Op.mult, ["tF", "SAME"], ["WC"])
+    for (base, par) in ((20, 27), (23, 26)):
+        later(ts, T.KF[:, base:base + 3], T.KF[:, 30:33], cf(par), None, Op.mult, None, [kk(30), kk(31), kk(32), kk(par)], [kk(base)])
+
+    def buf(n, b): return T[n + "%d" % b]
+    def key(n, b): return "%s%d" % (n, b)
+    def xread(t): return ["X", "Xd"] + (["Xown0", "Xarr0"] if t else [])
+    def xwin(t): return T.X[:, GB:N0 + W + K * t]
+    def awin(t): return T.A[:, GB:N0 + W + K * t]
+    def vo(b): return T.VO[:, 8 * b:8 * b + 8]
+    def wb(b): return slice(128 * b, 128 * b + 128)
+
+    def links(t, b):
+        op("V", lambda: v.tensor_scalar(buf("AO", b)[:], awin(t).indirect(vo(b)), 8, None, Op.add),
+           ["A", "Ad", "Anew0", "Anew1", key("VO", b)], [key("AO", b)])
+
+    def numbers(t, b, hs=(0, 1)):
+        for h in hs:
+            ac(buf("D", b)[:, 1024 * h:1024 * h + 1024], xwin(t).indirect(buf("AO", b)[:, 64 * h:64 * h + 64]), AF.Copy,
+               [key("AO", b)] + xread(t), ["D%d%d" % (b, h)])
+
+    def half(b):
+        cp(buf("AH", b)[:], buf("AO", b)[:], [key("AO", b)], [key("AH", b)])
+
+    def gather_y(t, b):
+        cp(T.Y[:, wb(b)], xwin(t).indirect(vo(b)), [key("VO", b)] + xread(t), [key("Y", b)])
+
+    def halve(b):
+        o = buf("ch", b)[:, 384:512]
+        mm(o, T.WR[:, 0:128], buf("Z", b)[:], True, False, ["WR", key("Z", b)], key("ch", b))
+        mm(o, T.WR[:, 0:128], T.Y[:, wb(b)], False, True, ["WR", key("Y", b)], key("ch", b))
+
+    def new_z(b):
+        ts(buf("Z", b)[:], buf("ch", b)[:, 384:512], MAGIC, MAGIC, Op.add, Op.subtract, [key("ch", b)], [key("Z", b)])
+
+    def spread_z(b):
+        for r in range(KZ):
+            mm(buf("zp", b)[:, r::KZ], T.IB[:], buf("Z", b)[:], True, True, ["IB", key("Z", b)], key("zp", b))
+        mm(buf("dist", b)[:, 0:128], buf("Z", b)[:], T.ZM[:], True, False, ["ZM", key("Z", b)], key("dist", b))
+
+    def bar(b, k):
+        for k2 in range(k):
+            mm(buf("dist", b)[:, 0:128], buf("SA", b)[:, wb(k2)], T.TRI[:], False, False, ["TRI", key("SA", b)], key("dist", b))
+
+    def sums_d(t, b):
+        for i in range(15):
+            w = T.B1 if (t == 0 and i == 14) else T.BN
+            mm(buf("dist", b)[:, 14 - i:128:16], buf("D", b)[:, i::16], w[:], False, False, ["B1", "BN", "D%d0" % b, "D%d1" % b], key("dist", b))
+
+    PLAN = [[[(0, 4)], [(1, 4)], [(2, 8), (6, 16)], [(3, 8), (7, 16)]], [[(0, 4)], [(1, 4)], [(2, 4)], [(3, 8), (7, 16)]]]
+
+    def max_op(t, b, h, j):
+        for (a, st) in PLAN[t][j]:
+            r = slice(1024 * h + a, 1024 * h + 1024, st)
+            tt(buf("M", b)[:, r], buf("D", b)[:, r], buf("zp", b)[:, 256 * h:256 * h + 256:st // 4], Op.max, ["D%d%d" % (b, h), key("zp", b)], ["M%d%d%d" % (b, h, a)])
+
+    def sums_m(t, b, j):
+        for (a, st) in PLAN[t][j]:
+            for i in range(a, 16, st):
+                mm(buf("dist", b)[:, 14 - i:128:16], buf("M", b)[:, i::16], T.B2[:], False, i == 7,
+                   ["B2", "M%d0%d" % (b, a), "M%d1%d" % (b, a)], key("dist", b))
+
+    def sel_a(b):
+        ts(buf("NV", b)[:], buf("dist", b)[:, 0:128], 65.5, None, Op.is_ge, None, [key("dist", b)], [key("NV", b)])
+        op("V", lambda: v.tensor_tensor_scan(buf("NT", b)[:, 1:129], buf("NV", b)[:], T.DC[:], 1.0, Op.mult, Op.max), [key("NV", b), "DC"], [key("NT", b)])
+        o = buf("ch", b)[:, 0:128]
+        mm(o, T.PERM[:], buf("AH", b)[:], True, False, ["PERM", key("AH", b)], key("ch", b))
+        mm(o, buf("NT", b)[:, 0:128], T.IP[:], False, False, ["IP", key("NTi", b), key("NT", b)], key("ch", b))
+        mm(o, buf("NT", b)[:, 1:129], T.IN[:], False, True, ["IN", key("NT", b)], key("ch", b))
+
+    def sel_b(b, k):
+        sa = buf("SA", b)[:, wb(k)]
+        ts(sa, buf("ch", b)[:, 0:128], cf(4), 0.0, Op.add, Op.max, [key("ch", b), kk(4)], [key("SA", b)])
+        mm(buf("ch", b)[:, 128:256], sa, T.BLK[:], True, True, ["BLK", key("SA", b)], key("ch", b))
+
+    def sel_c(b):
+        tt(buf("LT", b)[:], buf("ch", b)[:, 128:256], T.MK[:], Op.mult, [key("ch", b), "MK"], [key("LT", b)])
+        mm(buf("ch", b)[:, 256:264], buf("LT", b)[:], T.BH[:], True, True, ["BH", key("LT", b)], key("ch", b))
+
+    def sel_d(b):
+        cp(vo(b), buf("ch", b)[:, 256:264], [key("ch", b)], [key("VO", b)])
+
+    def bits1(b):
+        for lo in (128, 256):
+            o = buf("dist", b)[:, lo:lo + 128]
+            mm(o, T.IH[:], T.CT[:, wb(b)], True, False, ["IH", "CT"], key("dist", b))
+            mm(o, T.WB[:], buf("SA", b)[:, wb(4)], False, lo == 128, ["WB", key("SA", b)], key("dist", b))
+
+    def bits2(b):
+        ts(buf("HH", b)[:], buf("dist", b)[:, 128:256], MAGIC, MAGIC, Op.add, Op.subtract, [key("dist", b)], [key("HH", b)])
+
+    def vote(b):
+        tt(T.GT[:, wb(b)], T.Y[:, wb(b)], buf("zp", b)[:, 0::KZ], Op.is_gt, [key("Y", b), key("zp", b)], [key("GT", b)])
+        o = buf("dist", b)[:, 256:384]
+        mm(o, T.WH[:], buf("HH", b)[:], False, False, ["WH", key("HH", b)], key("dist", b))
+        mm(o, T.WC[:], T.GT[:, wb(b)], False, True, ["WC", key("GT", b)], key("dist", b))
+
+    def bits3(b):
+        ts(T.RB[:, wb(b)], buf("dist", b)[:, 256:384], 0.0, 0.5, Op.is_gt, Op.subtract, [key("dist", b)], [key("RB", b)])
+
+    def left(b, q):
+        for (nm, base) in (("LE", 20), ("LO", 23)):
+            if q == "V":
+                ts(T[nm][:, wb(b)], T.RB[:, wb(b)], cf(base), cf(base + 1 + b), Op.mult, Op.add, [key("RB", b), kk(base)], [key(nm, b)])
+            else:
+                ac(T[nm][:, wb(b)], T.RB[:, wb(b)], AF.Identity, [key("RB", b), kk(base)], [key(nm, b)], scale=cf(base), bias=cf(base + 1 + b))
+
+    def flipped(b):
+        ac(T.FY[:, wb(b)], T.Y[:, wb(b)], AF.Identity, [key("Y", b), kk(8), kk(9)], [key("FY", b)], scale=cf(8), bias=cf(9))
+
+    def turn(b):
+        for j in range(4):
+            d = (4 * b + j - rank) % 8
+            rot = T.WR[:, 128 - 16 * d:256 - 16 * d]
+            oo = buf("ch", b)[:, 384 + 32 * j:416 + 32 * j]
+            mm(oo, rot, buf("Z", b)[:, 32 * j:32 * j + 32], True, False, ["WR", key("Z", b)], key("ch", b))
+            mm(oo, rot, T.Y[:, 128 * b + 32 * j:128 * b + 32 * j + 32], False, True, ["WR", key("Y", b)], key("ch", b))
+
+    sent = [0]
+
+    def send(t, b):
+        zs, o = T["ZS%d" % t], buf("ch", b)
+        c0 = N0 + W + K * t + 32 * rank
+        ts(zs[:, wb(b)], o[:, 384:512], MAGIC, MAGIC, Op.add, Op.subtract, [key("ch", b)], ["ZS%d%d" % (t, b)])
+        if rank // 4 == b:
+            j = rank % 4
+            ts(T.X[:, c0:c0 + 32], o[:, 384 + 32 * j:416 + 32 * j], MAGIC, MAGIC, Op.add, Op.subtract, [key("ch", b)], ["Xown%d" % t])
+        deps("G", ["ZS%d%d" % (t, b)], [])
+        trs, used = [], set()
+        for q in sorted([q for q in range(4 * b, 4 * b + 4) if q != rank], key=lambda q: len(topo.engines(core, T.cores[q]))):
+            dst = T.cores[q]
+            es = topo.engines(core, dst)
+            es = es[0::2] + es[1::2]
+            if dst in topo.cores_of(core):
+                es = es[::-1]
+            e = [x for x in es if x not in used][0]
+            used.add(e)
+            rid, pid = topo.addr(dst, core)
+            trs.append(RemoteDMATransfer(dst_ids=[DstId(rid=rid, pnc=pid)], dma_engine_mask=1 << e, remote_sem=sem["arr%d" % t],
+                                         src=zs[:, 32 * q:32 * q + 32], dst=T.X[:, c0:c0 + 32]))
+        g.remote_dma_fused(trs, local_sem=sem["snt"])
+        sent[0] += len(trs)
+
+    def pairs(bk, lo, gg, c, first, last, kb):
+        a, nm = gg // 2, "LE" if gg % 2 == 0 else "LO"
+        tri = first <= 128 * c < last
+        mm(bk[:, lo:lo + last - first], T[nm][32 * a:32 * a + 32, wb(c)], T.RB[32 * a:32 * a + 32, first:last], True, not tri,
+           [key(nm, c), "RB0"] + (["RB1"] if last > 128 else []), kb)
+        if tri:
+            mm(bk[:, lo + 128 * c - first:lo + 128 * c - first + 128], T.IB[:], T.T2[:], False, True, ["IB", "T2"], kb)
+
+    def reduce_v(src, j, kb):
+        op("V", lambda: v.tensor_reduce(T.ACV[:, j:j + 1], src, AxisListType.X, Op.max), [kb], ["ACV%d" % j])
+
+    def reduce_s(src, n, j, kb):
+        o = 256 * (j % 4)
+        ac(T.junk[:, o:o + n], src, AF.Relu, [kb], ["ACS%d" % j, "junk%d" % (j % 4)], accum_out=T.ACS[:, j:j + 1])
+
+    def place_v(nm, gg, j, an):
+        ts(T[nm][:, 16 * gg:16 * gg + 16], T.M5[:], T[an][:, j:j + 1], 0.0, Op.min, Op.max, ["M5", "%s%d" % (an, j)], ["%s%d" % (nm, gg)])
+
+    def place_s(nm, gg, j):
+        ac(T[nm][:, 16 * gg:16 * gg + 16], T.MN[:], AF.Relu, ["MN", "ACS%d" % j], ["%s%d" % (nm, gg)], bias=T.ACS[:, j:j + 1])
+
+    def early(gs):
+        kbs = ["eA", "eB", "dist0", "zp0"]
+        for gg in gs:
+            pairs(T[kbs[gg // 2]], 128 * (gg % 2), gg, 0, 0, 128, kbs[gg // 2])
+        for gg in gs:
+            reduce_s(T[kbs[gg // 2]][:, 128 * (gg % 2):128 * (gg % 2) + 128], 128, gg, kbs[gg // 2])
+
+    def new_links(t, b):
+        op("V", lambda: v.tensor_tensor(T.VAL[:, wb(b)], awin(t).indirect(vo(b)), T.AD[:, wb(b)], Op.max), ["A", "Ad", key("VO", b), "AD"], [key("VAL", b)])
+        ts(T.A[:, N0 + W + 128 * b:N0 + W + 128 * b + 128], T.VAL[:, wb(b)], m16(15), cf(11), Op.mult, Op.add, [key("VAL", b), "M16", kk(11)], [key("Anew", b)])
+
+    def final_nodes(b):
+        mm(buf("ch", b)[:, 128:256], T.BLK[:], buf("SA", b)[:, wb(4)], True, True, ["BLK", key("SA", b)], key("ch", b))
+        ts(T.YV[:, wb(b)], buf("ch", b)[:, 128:256], 8.0, None, Op.subtract, None, [key("ch", b)], [key("YV", b)])
+
+    def late(t):
+        banks = [("eA", T.eA), ("eB", T.eB), ("dist0", T.dist0), ("dist1", T.dist1)]
+        for p in range(4):
+            for gg in (2 * p, 2 * p + 1):
+                kb, bk = banks[gg % 4]
+                pairs(bk, 0, gg, 0, 128, 256, kb)
+                pairs(bk, 256, gg, 1, 0, 256, kb)
+            if t and p < 2:
+                final_nodes(p)
+            for gg in (2 * p, 2 * p + 1):
+                kb, bk = banks[gg % 4]
+                if gg in (1, 3, 4, 6):
+                    reduce_s(bk[:, 0:128], 128, 8 + 2 * gg, kb)
+                    reduce_s(bk[:, 256:512], 256, 9 + 2 * gg, kb)
+                    place_s("LAB", gg, 8 + 2 * gg)
+                    place_s("LBB", gg, 9 + 2 * gg)
+                else:
+                    reduce_v(bk[:, 0:128], 2 * gg, kb)
+                    reduce_v(bk[:, 256:512], 2 * gg + 1, kb)
+                    place_v("LAB", gg, 2 * gg, "ACV")
+                    place_v("LBB", gg, 2 * gg + 1, "ACV")
+        ra, rb, rc = [["%s%d" % (nm, gg) for gg in range(8)] for nm in ("LAA", "LAB", "LBB")]
+        for (lo, w, wn) in (((256, T.B1, "B1"),) if t == 0 else ()) + ((288, T.B4, "B4"),):
+            oa, ob = T.ch0[:, lo:lo + 8], T.ch0[:, lo + 8:lo + 16]
+            isx = wn == "B4"
+            if isx:
+                mm(oa, T.LT0[:], T.BH[:], True, False, ["BH", "LT0"], "ch0")
+            mm(oa, T.LAA[:], w[:], not isx, False, [wn] + ra, "ch0")
+            mm(oa, T.LAB[:], w[:], False, True, [wn] + rb, "ch0")
+            if isx:
+                mm(ob, T.LT1[:], T.BH[:], True, False, ["BH", "LT1"], "ch0")
+            mm(ob, T.LBB[:], w[:], not isx, True, [wn] + rc, "ch0")
+        if t == 0:
+            ts(T.FR[:], T.ch0[:, 256:272], 511.5, -4096.0, Op.is_ge, Op.mult, ["ch0"], ["FR"])
+        tt(T.FF[:], T.ch0[:, 288:304], T.TR[:], Op.max, ["ch0", "TR"], ["FF"])
+        if t == 0:
+            tt(T.FR[:], T.FR[:], T.DV[:], Op.add, ["FR", "DV"], ["FR"])
+        ts(T.OFX[:], T.FF[:], float(GB), None, Op.add, None, ["FF"], ["OFX"])
+        if t == 0:
+            tt(T.FR[:], T.FR[:], T.TR[:], Op.max, ["FR", "TR"], ["FR"])
+            ts(T.OFA[:], T.FR[:], float(GB), None, Op.add, None, ["FR"], ["OFA"])
+            cp(T.A[:, 0:N0 + W].indirect(T.OFA[:]), T.VAL[:], ["OFA", "VAL0", "VAL1", "Ad"], ["A"])
+
+    def flip(t):
+        cp(T.X[:, 0:N0 + W + K * t].indirect(T.OFX[:]), T.FY[:], ["OFX", "FY0", "FY1", "Xd"] + (["Xown0", "Xarr0"] if t else []), ["X"])
+
+    for t in range(RO):
+        lastw["Xarr%d" % t] = [("arr%d" % t, 7)]
+        links(t, 0)
+        if t:
+            flip(0)
+        numbers(t, 0, (1,))
+        links(t, 1)
+        numbers(t, 1)
+        for b in range(2):
+            cp(buf("Z", b)[:], xwin(t).indirect(vo(b)), [key("VO", b)] + xread(t), [key("Z", b)])
+            spread_z(b)
+            if b == 0:
+                cp(T.D0[:, 0:1024], xwin(t).indirect(T.AO0[:, 0:64]), ["AO0"] + xread(t), ["D00"])
+        half(0)
+        half(1)
+        for j in range(4):
+            max_op(t, 0, 0, j)
+        pend = None
+        for k in range(S):
+            for b in range(2):
+                last = (b, k) == (1, S - 1)
+                nb = 1 - b
+
+                def fill(*js):
+                    for j in js:
+                        if not last:
+                            max_op(t, nb, 0, j)
+                sums_d(t, b)
+                if last:
+                    bits2(0)
+                for j in range(4):
+                    max_op(t, b, 1, j)
+                    sums_m(t, b, j)
+                if pend:
+                    gather_y(t, nb)
+                    halve(nb)
+                    half(nb)
+                sel_a(b)
+                if pend:
+                    new_z(nb)
+                    spread_z(nb)
+                if last:
+                    vote(0)
+                for f in deferred[:4]:
+                    f()
+                del deferred[:4]
+                sel_b(b, k)
+                if last:
+                    turn(0)
+                    bits1(1)
+                    bits3(0)
+                    left(0, "S")
+                    flipped(0)
+                    if t == 0:
+                        new_links(t, 0)
+                fill(0)
+                sel_c(b)
+                if last:
+                    send(t, 0)
+                    bits2(1)
+                    early(range(0, 4))
+                fill(1, 2)
+                if pend:
+                    bar(*pend)
+                pend = None
+                sel_d(b)
+                if k < S - 1:
+                    links(t, b)
+                    numbers(t, b)
+                    pend = (b, k + 1)
+                    fill(3)
+                elif b == 0:
+                    bits1(0)
+                    ac(T.Y[:, wb(0)], xwin(t).indirect(vo(0)), AF.Copy, ["VO0"] + xread(t), ["Y0"])
+                    fill(3)
+                else:
+                    gather_y(t, 1)
+                    vote(1)
+                    bits3(1)
+                    left(1, "V")
+                    early(range(4, 8))
+                    turn(1)
+                    flipped(1)
+                    if t == 0:
+                        ts(T.DV[:], T.VO[:], 1.0, None, Op.mult, None, ["VO0", "VO1"], ["DV"])
+                    send(t, 1)
+                    if t == 0:
+                        new_links(t, 1)
+                    for gg in range(8):
+                        place_v("LAA", gg, gg, "ACS")
+                    late(t)
+    flip(RO - 1)
+    deps("S", ["X", "Xd", "Xown0", "Xarr0"], [])
+    act.dma_start(T.yx[:, 0:W + K], T.X[:, N0:N0 + W + K]).then_inc(sem.out2, 16)
+    deps("Y", ["YV0", "YV1"], [])
+    g.sync.dma_start(T.yv[:], T.YV[0::16, :]).then_inc(sem.out1, 16)
+    deps("Y", ["Xown1", "Xarr1"], [])
+    g.sync.dma_start(T.yx[:, W + K:W + 2 * K], T.X[:, N0 + W + K:N0 + W + 2 * K]).then_inc(sem.out3, 16)
+    for s, n in (("qV", cnt["V"]), ("qP", cnt["P"]), ("qS", cnt["S"]), ("qG", cnt["G"]), ("snt", sent[0]), ("arr0", 7), ("arr1", 7),
+                 ("out1", 16), ("out2", 16), ("out3", 16), ("ldw", 16), ("ldx", 16), ("ldal", 64), ("ldas", 64), ("ldn", 16)):
+        g.wait_ge(sem[s], n)

@@ -3,12 +3,25 @@ from concourse.bass import DstId, RemoteDMATransfer
 from concourse.mybir import dt, AluOpType as Op, AxisListType, ActivationFunctionType as AF
 
 W, K, RO, S = 1664, 256, 2, 5
-GB = 256
+GB = 128
 N0 = GB + 8
-XC = N0 + W + RO * K
 AC = N0 + W + K
 MAGIC = 12582912.0
-KZ = 4
+U = 4096.0
+VS = 16
+FILL = (48, 0)
+SCUT = (64, 96)
+PIECES = {"A": (0, 64, 0, 4), "B": (0, 64, 1, 4), "C": (0, 64, 2, 4), "D": (0, 64, 3, 4),
+          "E": (64, 96, 0, 2), "F": (64, 96, 1, 2), "G": (96, 128, 0, 2), "H": (96, 128, 1, 2)}
+PLAN = ("GHzv", "1AB", "bC", "Dh", "E", "F")
+ENG = (2, 4)
+ARR = 4 * ENG[0] + 3 * ENG[1]
+DIAG = ("SVSSVSSV", "VVSVVSVV")
+SUMS = {"l0": "S", "k0": "VS", "l1": "S", "k1": "VS"}
+PART = {"k": slice(0, 8), "l": slice(8, 16)}
+FIX = {"V": 40, "S": 50, "P": 0, "G": 180, "Y": 100}
+GATHER, SCATTER, HOP, DMA, PE = 1.56, 3.8, 160, 2500, 0.6
+PASSES = 4
 
 SCRATCH = {}
 
@@ -18,31 +31,72 @@ def declare(where, dtype, names, shape):
         SCRATCH[nm] = (where, shape, dtype)
 
 
-declare("sbuf", "bfloat16", "X", [128, XC])
+declare("sbuf", "bfloat16", "X", [128, AC + 8])
+declare("sbuf", "bfloat16", "F0 F1", [128, AC])
 declare("sbuf", "int32", "A", [128, AC])
 declare("sbuf", "int32", "w0s KI", [128, 16])
-declare("sbuf", "uint16", "VO OFX OFA", [128, 16])
-declare("sbuf", "bfloat16", "Y GT FY RB LE LO ZS0 ZS1 ZERO WR", [128, 256])
-declare("sbuf", "bfloat16", "junk", [128, 1024])
-declare("sbuf", "float32", "VAL YV AD cF", [128, 256])
-declare("sbuf", "float32", "ACV DV FF FR M16 M5 MN TR", [128, 16])
-declare("sbuf", "float32", "ACS", [128, 32])
+declare("sbuf", "uint16", "VO OF0 OF1", [128, 16])
+declare("sbuf", "bfloat16", "XA ZS0 ZS1 ZERO WR", [128, 256])
+declare("sbuf", "bfloat16", "junk", [128, 512])
+declare("sbuf", "float32", "YV AD cF", [128, 256])
+declare("sbuf", "float32", "M16 TR AC0 AC1 FF0 FF1 VF0 VF1", [128, 16])
+declare("sbuf", "float32", "WI CVS CVVS SC BI", [128, 8])
 declare("sbuf", "float32", "KF", [128, 40])
-declare("sbuf", "bfloat16", "LAA LAB LBB IB IP IN ZM MK DC WC T2 Z0 Z1 NV0 NV1", [128, 128])
-declare("sbuf", "float16", "IH TRI PERM BLK WB WH AH0 AH1 LT0 LT1 HH0 HH1", [128, 128])
+declare("sbuf", "bfloat16", "IB IP IN ZM0 ZM1 MK DC WC WS I75 C75 Z0 Z1 SY0 SY1 Y0 Y1 YC GT0 GT1 Rl0 Rl1 Rk0 Rk1 SG0 SG1 FG TV0 TV1 ZT", [128, 128])
+declare("sbuf", "bfloat16", "BD0 BD1", [128, 8, 128])
+declare("sbuf", "float16", "IH I4 TRI PERM BLK WB WB4 WH4 CT AH0 AH1 LT0 LT1 HH0 HH1", [128, 128])
 declare("sbuf", "float32", "tF SAME PW", [128, 128])
-declare("sbuf", "int32", "cmI cgI", [128, 128])
-declare("sbuf", "int32", "cI", [128, 256])
+declare("sbuf", "int32", "cI cmI cgI VAL0 VAL1", [128, 128])
 declare("sbuf", "int32", "pI", [128, 1])
-declare("sbuf", "bfloat16", "B2 BN B1 B4", [128, 8])
+declare("sbuf", "bfloat16", "B2 BN", [128, 8])
 declare("sbuf", "float16", "BH", [128, 8])
-declare("sbuf", "float16", "CT", [128, 256])
 declare("sbuf", "bfloat16", "D0 D1 M0 M1", [128, 2048])
 declare("sbuf", "uint16", "AO0 AO1", [128, 128])
 declare("sbuf", "bfloat16", "NT0 NT1", [128, 136])
 declare("sbuf", "float16", "SA0 SA1", [128, S * 128])
-declare("psum", "float32", "eA eB dist0 dist1 ch0 ch1 zp0 zp1", [128, 512])
-SEMAPHORES = ["qV", "qP", "qS", "qG", "ldw", "ldx", "ldal", "ldas", "ldn", "arr0", "arr1", "snt", "out1", "out2", "out3"]
+BANKS = "dist0 dist1 ch0 ch1 zp00 zp01 zp10 zp11".split()
+declare("psum", "float32", "dist0 dist1 ch0 ch1", [128, 512])
+declare("psum", "float32", "zp00 zp01 zp10 zp11", [128, 64, 8])
+SEMAPHORES = ["qV", "qP", "qS", "qG", "ldw", "ldx", "ldal", "ldas", "ldn", "arr0", "arr1", "snt", "out1", "out2", "out3", "out4", "suc0", "suc1"]
+
+
+def lay_out(calls):
+    n = len(calls)
+    after = [[] for _ in calls]
+    for i, c in enumerate(calls):
+        for j in c["before"]:
+            after[j].append(i)
+    tail = [0.0] * n
+    for i in reversed(range(n)):
+        tail[i] = calls[i]["cost"] + calls[i]["lat"] + max([tail[j] for j in after[i]] + [0.0])
+
+    def place(order, back):
+        busy, end = {c["q"]: [] for c in calls}, [0.0] * n
+        for i in order:
+            c = calls[i]
+            if back:
+                t = max([end[j] + (c["lat"] if calls[j]["before"][i] else 0) for j in after[i]] + [c["lat"]])
+            else:
+                t = max([end[j] + (calls[j]["lat"] if w else 0) for j, w in c["before"].items()] + [0.0])
+            row = busy[c["q"]]
+            at = len(row)
+            while at and row[at - 1][1] > t:
+                at -= 1
+            while at < len(row) and row[at][0] < t + c["cost"]:
+                t = max(t, row[at][1])
+                at += 1
+            end[i] = t + c["cost"]
+            row.insert(at, (t, end[i]))
+        return end
+    order, best = sorted(range(n), key=lambda i: (-tail[i], i)), None
+    for _ in range(PASSES):
+        end = place(order, False)
+        span = max(end[i] + calls[i]["lat"] for i in range(n))
+        if best is None or span < best[0]:
+            best = (span, sorted(range(n), key=lambda i: (end[i] - calls[i]["cost"], i)))
+        end = place(sorted(range(n), key=lambda i: (-end[i], -i)), True)
+        order = sorted(range(n), key=lambda i: (-end[i], i))
+    return best[1]
 
 
 def rank_program(g, core, T, topo):
@@ -51,492 +105,465 @@ def rank_program(g, core, T, topo):
         return
     sem = T.sem
     eng = {"V": g.vector, "P": g.tensor, "S": g.scalar, "G": g, "Y": g.sync}
-    qsem = {"V": "qV", "P": "qP", "S": "qS", "G": "qG"}
-    clock = {q: {} for q in eng}
-    cnt = {q: 0 for q in eng}
-    snap = {}
-    lastw, readers = {}, {}
+    calls, lastw, readers, chain = [], {}, {}, {"on": False, "V": None, "S": None, "P": None}
 
-    def need(q, tok):
-        s, n = tok
-        if clock[q].get(s, 0) >= n:
-            return
-        eng[q].wait_ge(sem[s], n)
-        c = clock[q]
-        for k2, v2 in snap.get(tok, {}).items():
-            if c.get(k2, 0) < v2:
-                c[k2] = v2
-        c[s] = n
-
-    def deps(q, reads, writes, acc=()):
-        own = qsem.get(q)
-        want = {}
+    def op(q, f, reads, writes, acc=(), cost=128, lat=HOP, tok=None):
+        before = {}
         for k in reads:
-            for t in lastw.get(k, ()):
-                want[t[0]] = max(want.get(t[0], 0), t[1])
+            for j in lastw.get(k, []) + [j for j in readers.get(k, []) if k in BANKS and calls[j]["q"] != q]:
+                before[j] = True
         for k in list(writes) + list(acc):
-            for t in list(lastw.get(k, ())) + list(readers.get(k, ())):
-                if t[0] != own or (k not in acc and t in lastw.get(k, ())):
-                    want[t[0]] = max(want.get(t[0], 0), t[1])
-        for s, n in want.items():
-            need(q, (s, n))
-
-    def op(q, f, reads, writes, acc=()):
-        deps(q, reads, writes, acc)
-        f().then_inc(sem[qsem[q]], 1)
-        cnt[q] += 1
-        tok = (qsem[q], cnt[q])
-        snap[tok] = dict(clock[q])
+            for j in lastw.get(k, []):
+                before[j] = before.get(j, False) or calls[j]["q"] != q or k not in acc
+            for j in readers.get(k, []):
+                before[j] = before.get(j, False) or calls[j]["q"] != q or calls[j]["tok"] is not None
+        if q in chain and chain["on"]:
+            if chain[q] is not None:
+                before.setdefault(chain[q], False)
+            chain[q] = len(calls)
+        calls.append({"q": q, "f": f, "before": before, "cost": FIX.get(q, 0) + cost, "lat": lat, "tok": tok})
         for k in list(writes) + list(acc):
-            lastw[k] = [tok]
-            readers[k] = []
+            lastw[k], readers[k] = [len(calls) - 1], []
         for k in reads:
-            readers.setdefault(k, []).append(tok)
+            readers.setdefault(k, []).append(len(calls) - 1)
 
-    def load(f, name, total, k):
-        f().then_inc(sem[name], 16)
-        lastw[k] = [t for t in lastw.get(k, []) if t[0] != name] + [(name, total)]
+    def dma(q, out, in_, name, total, reads, writes, lat=DMA):
+        op(q, lambda: eng[q].dma_start(out, in_).then_inc(sem[name], 16), reads, writes, ["dma" + q], cost=0, lat=lat, tok=[(name, total)])
 
     v, pe, act = g.vector, g.tensor, g.scalar
 
-    def ts(out, in0, s1, s2, o0, o1, reads, writes):
+    def ts(out, in0, s1, s2, o0, o1, reads, writes, c=128):
         if o1 is None:
-            op("V", lambda: v.tensor_scalar(out, in0, s1, None, o0), reads, writes)
+            op("V", lambda: v.tensor_scalar(out, in0, s1, None, o0), reads, writes, cost=c)
         else:
-            op("V", lambda: v.tensor_scalar(out, in0, s1, s2, o0, o1), reads, writes)
+            op("V", lambda: v.tensor_scalar(out, in0, s1, s2, o0, o1), reads, writes, cost=c)
 
-    def tt(out, a, b, o, reads, writes):
-        op("V", lambda: v.tensor_tensor(out, a, b, o), reads, writes)
+    def tt(out, a, b, o, reads, writes, c=128):
+        op("V", lambda: v.tensor_tensor(out, a, b, o), reads, writes, cost=c)
 
-    def cp(out, in_, reads, writes):
-        op("V", lambda: v.tensor_copy(out, in_), reads, writes)
+    def cp(out, in_, reads, writes, c=128):
+        op("V", lambda: v.tensor_copy(out, in_), reads, writes, cost=c)
 
-    def ac(out, in_, f, reads, writes, **kw):
-        op("S", lambda: act.activation(out, in_, f, **kw), reads, writes)
+    def fill(out, x, reads, k, c=8):
+        op("V", lambda: v.memset(out, x), reads, [k], cost=c)
 
-    def lin(out, in_, scale, bias, reads, k):
-        ac(out, in_, AF.Copy if isinstance(bias, float) else AF.Identity, reads, [k], scale=scale, bias=bias)
+    def ac(out, in_, f, reads, writes, c=128, **kw):
+        op("S", lambda: act.activation(out, in_, f, **kw), reads, writes, cost=c)
 
-    def mm(out, l, r, start, stop, reads, key):
-        op("P", lambda: pe.matmul(out, l, r, start, stop), reads, (), (key,))
+    def lin(out, in_, scale, bias, reads, k, c=128):
+        ac(out, in_, AF.Copy if isinstance(bias, float) else AF.Identity, reads, [k], c, scale=scale, bias=bias)
 
-    load(lambda: g.sync.dma_start(T.w0s[:], T.w0[:]), "ldw", 16, "w0s")
-    for gg in range(4):
-        load(lambda: g.sync.dma_start(T.A[16 * gg:16 * gg + 15, N0:N0 + W], T.lk[16 * gg:16 * gg + 15, :]), "ldal", 64, "A")
-    for gg in range(4, 8):
-        load(lambda: act.dma_start(T.A[16 * gg:16 * gg + 15, N0:N0 + W], T.lk[16 * gg:16 * gg + 15, :]), "ldas", 64, "A")
-    load(lambda: g.sync.dma_start(T.A[15::16, N0:N0 + W], T.nx[:]), "ldn", 16, "A")
-    load(lambda: act.dma_start(T.X[:, N0:N0 + W], T.x0[:]), "ldx", 16, "X")
+    def mm(out, l, r, start, stop, reads, key, c=128):
+        op("P", lambda: pe.matmul(out, l, r, start, stop), reads, (), (key,), cost=c * PE)
 
-    op("G", lambda: g.iota(T.pI[:], [[0, 1]], 0, 1), [], ["pI"])
-    op("G", lambda: g.iota(T.cI[:], [[1, 256]], 0, 0), [], ["cI"])
-    op("V", lambda: v.memset(T.ZERO[:], 0.0), [], ["ZERO"])
+    dma("Y", T.w0s[:], T.w0[:], "ldw", 16, [], ["w0s"])
+    dma("S", T.A[0::2, N0:N0 + W], T.lk[0::2, :], "ldas", 16, [], ["A0"], 2 * DMA)
+    for a, st in ((1, 4), (3, 8), (7, 16)):
+        dma("Y", T.A[a::st, N0:N0 + W], T.lk[a::st, :], "ldal", 48, [], ["A%d" % a], 2 * DMA)
+    dma("Y", T.A[15::16, N0:N0 + W], T.nx[:], "ldn", 16, [], ["A15"], 2 * DMA)
+    dma("S", T.X[:, N0:N0 + W], T.x0[:], "ldx", 16, [], ["X"], 2 * DMA)
+    op("", None, ["A0", "A1", "A3", "A7", "A15"], ["A"], cost=0, lat=0, tok=[("ldas", 16), ("ldal", 48), ("ldn", 16)])
 
-    def stripe(nm, n, cmp, fill, base, step, cm, again=False):
-        op("G", lambda: g.affine_select(T[nm][:], T[nm][:] if again else T.ZERO[:, 0:n], [[step, n]], cmp, fill, base, cm), [nm] if again else ["ZERO"], [nm])
-    stripe("IB", 128, Op.not_equal, 1.0, 0, -1, 1)
-    stripe("IP", 128, Op.not_equal, 2048.0, 0, -1, 1)
-    stripe("IN", 128, Op.not_equal, -2048.0, 0, -1, 1)
-    stripe("WR", 256, Op.not_equal, 63.0 / 128, 0, -1, 1)
-    stripe("WR", 256, Op.not_equal, 63.0 / 128, 128, -1, 1, True)
-    stripe("T2", 128, Op.is_ge, 512.0, 0, 1, -1)
-    op("G", lambda: g.iota(T.cF[:], [[1, 256]], W, 0, allow_small_or_imprecise_dtypes=True), [], ["cF"])
-    op("V", lambda: v.memset(T.X[:, GB:N0], 127.0), [], ["Xd"])
-    op("V", lambda: v.memset(T.A[:, GB:N0], -1), [], ["Ad"])
-    op("V", lambda: v.memset(T.NT0[:, 0:1], 1.0), [], ["NTi0"])
-    op("V", lambda: v.memset(T.NT1[:, 0:1], 1.0), [], ["NTi1"])
-    op("V", lambda: v.memset(T.PW[:], 0.0), [], ["PW"])
+    op("G", lambda: g.iota(T.pI[:], [[0, 1]], 0, 1), [], ["pI"], cost=2)
+    op("G", lambda: g.iota(T.cI[:], [[1, 128]], 0, 0), [], ["cI"], cost=256)
+    op("G", lambda: g.iota(T.cF[:], [[1, 256]], 0, 0, allow_small_or_imprecise_dtypes=True), [], ["cF"], cost=512)
+    fill(T.ZERO[:], 0.0, [], "ZERO", 128)
 
+    def stripe(nm, n, x, base, again=False):
+        op("G", lambda: g.affine_select(T[nm][:], T[nm][:] if again else T.ZERO[:, 0:n], [[-1, n]], Op.not_equal, x, base, 1),
+           [nm] if again else ["ZERO"], [nm], cost=2 * n)
+    stripe("IB", 128, 1.0, 0)
+    stripe("IP", 128, 2048.0, 0)
+    stripe("IN", 128, -2048.0, 0)
+    stripe("WR", 256, 63.0 / 128, 0)
+    stripe("WR", 256, 63.0 / 128, 128, True)
+    op("G", lambda: g.iota(T.A[:, N0 + W:AC], [[0, K]], -1, 0), ["WR"], ["Af"], cost=2 * K)
+    for t in range(RO):
+        op("G", lambda t=t: g.iota(T["F%d" % t][:, GB:AC], [[0, AC - GB]], -1, 0, allow_small_or_imprecise_dtypes=True), ["WR"], ["F%d" % t], cost=2 * AC)
+    fill(T.X[:, GB:N0], 127.0, [], "Xd")
+    fill(T.X[:, AC:AC + 8], 127.0, [], "Xe")
+    fill(T.A[:, GB:N0], -1, [], "Ad")
+    fill(T.NT0[:, 0:1], 66.0, [], "NTi0")
+    fill(T.NT1[:, 0:1], 66.0, [], "NTi1")
+    fill(T.PW[:], 0.0, [], "PW", 128)
+
+    names = {}
+
+    def cf(n): return T.KF[:, names.setdefault(n, len(names)):names[n] + 1]
     def ci(j): return T.KI[:, j:j + 1]
-    def cf(j): return T.KF[:, j:j + 1]
-    def kk(j): return "KF%d" % j
     def m16(j): return T.M16[:, j:j + 1]
-    ts(ci(0), T.pI[:], 15, None, Op.bitwise_and, None, ["pI"], ["KI0"])
-    ts(ci(1), T.pI[:], 4, None, Op.arith_shift_right, None, ["pI"], ["KI1"])
-    ts(ci(4), T.pI[:], 1, None, Op.bitwise_and, None, ["pI"], ["KI4"])
-    cp(cf(0), T.pI[:], ["pI"], [kk(0)])
-    cp(cf(1), ci(0), ["KI0"], [kk(1)])
-    cp(cf(2), ci(1), ["KI1"], [kk(2)])
-    ts(ci(5), ci(1), 1, None, Op.bitwise_and, None, ["KI1"], ["KI5"])
-    ts(T.cmI[:], T.cI[:, 0:128], 15, None, Op.bitwise_and, None, ["cI"], ["cmI"])
-    ts(T.cgI[:], T.cI[:, 0:128], 4, None, Op.arith_shift_right, None, ["cI"], ["cgI"])
-    P0, PM, PG = cf(0), cf(1), cf(2)
-    c128 = T.cI[:, 0:128]
-    ts(T.M16[:], T.cI[:, 0:16], PM, None, Op.is_equal, None, ["cI", kk(1)], ["M16"])
-    ts(cf(14), PM, 10.5, -1.5 + 2.0 ** -12, Op.is_lt, Op.mult, [kk(1)], [kk(14)])
+
+    def col(n, row, scale, plus):
+        lin(cf(n), m16(row), scale, plus if isinstance(plus, float) else cf(plus), ["M16"] + ([] if isinstance(plus, float) else [plus]), n, 1)
+    ts(ci(0), T.pI[:], 15, None, Op.bitwise_and, None, ["pI"], ["KI0"], 1)
+    ts(ci(1), T.pI[:], 4, None, Op.arith_shift_right, None, ["pI"], ["KI1"], 1)
+    ts(ci(4), T.pI[:], 1, None, Op.bitwise_and, None, ["pI"], ["KI4"], 1)
+    cp(cf("P0"), T.pI[:], ["pI"], ["P0"], 1)
+    cp(cf("PM"), ci(0), ["KI0"], ["PM"], 1)
+    cp(cf("PG"), ci(1), ["KI1"], ["PG"], 1)
+    ts(T.cmI[:], T.cI[:], 15, None, Op.bitwise_and, None, ["cI"], ["cmI"])
+    ts(T.cgI[:], T.cI[:], 4, None, Op.arith_shift_right, None, ["cI"], ["cgI"])
+    P0, PM, PG = cf("P0"), cf("PM"), cf("PG")
+    c128, c8 = T.cI[:], T.cI[:, 0:8]
+    ts(T.M16[:], T.cI[:, 0:16], PM, None, Op.is_equal, None, ["cI", "PM"], ["M16"], 16)
+    ts(cf("low"), PM, 10.5, None, Op.is_lt, None, ["PM"], ["low"], 1)
     ts(T.tF[:], T.cmI[:], 14.5, -1.0, Op.is_lt, Op.mult, ["cmI"], ["tF"])
-    ts(T.SAME[:], T.cgI[:], PG, None, Op.is_equal, None, ["cgI", kk(2)], ["SAME"])
-    for nm, f in (("B2", 2.0), ("BN", -1.0), ("B1", 1.0), ("BH", 1.0), ("B4", -4096.0)):
-        ts(T[nm][:], T.cI[:, 0:8], PG, f, Op.is_equal, Op.mult, ["cI", kk(2)], [nm])
-    tt(T.ZM[:], T.tF[:], T.SAME[:], Op.mult, ["tF", "SAME"], ["ZM"])
-    ts(T.DC[:], T.cmI[:], 15, None, Op.is_equal, None, ["cmI"], ["DC"])
-    lin(cf(6), PM, 1.0, -256.0, [kk(1)], kk(6))
-    lin(cf(15), m16(11), 7.5, 1.0, ["M16"], kk(15))
-    lin(cf(13), m16(13), -1.0, 0.0, ["M16"], kk(13))
-    lin(cf(16), m16(13), 126.5, cf(15), ["M16", kk(15)], kk(16))
-    lin(cf(18), cf(16), 1.0, cf(14), [kk(16), kk(14)], kk(18))
-    lin(cf(11), m16(15), 1.0, -1.0, ["M16"], kk(11))
-    lin(cf(12), m16(14), 1.0, -1.0, ["M16"], kk(12))
-    lin(cf(29), m16(12), -11264.0, m16(11), ["M16"], kk(29))
-    lin(cf(28), m16(13), 1.0, m16(15), ["M16"], kk(28))
-    lin(cf(31), cf(29), 1.0, m16(14), ["M16", kk(29)], kk(31))
-    lin(cf(32), cf(28), 512.0, cf(31), [kk(28), kk(31)], kk(32))
-    lin(T.M5[:], T.M16[:], 512.0, 0.0, ["M16"], "M5")
-    lin(T.MN[:], T.M16[:], 1e6, -1e6, ["M16"], "MN")
-    lin(T.AD[:], T.cF[:], m16(14), cf(12), ["cF", "M16", kk(12)], "AD")
-    ts(ci(2), ci(0), -1, 30, Op.mult, Op.add, ["KI0"], ["KI2"])
-    tt(cf(3), P0, PM, Op.subtract, [kk(0), kk(1)], [kk(3)])
-    ts(ci(3), ci(2), 15, None, Op.bitwise_and, None, ["KI2"], ["KI3"])
-    ts(cf(4), PM, 14.5, -2048.0, Op.is_lt, Op.mult, [kk(1)], [kk(4)])
-    tt(cf(5), ci(3), cf(3), Op.add, ["KI3", kk(3)], [kk(5)])
-    ts(T.BLK[:], T.cgI[:], PG, None, Op.is_equal, None, ["cgI", kk(2)], ["BLK"])
-    ts(T.PERM[:], c128, cf(5), None, Op.is_equal, None, ["cI", kk(5)], ["PERM"])
-    ts(T.MK[:], T.cmI[:], PM, None, Op.is_equal, None, ["cmI", kk(1)], ["MK"])
-    ts(cf(7), m16(15), -1000.0, P0, Op.mult, Op.add, ["M16", kk(0)], [kk(7)])
-    ts(T.tF[:], c128, cf(7), 1024.0, Op.is_le, Op.mult, ["cI", kk(7)], ["tF"])
-    tt(T.TRI[:], T.tF[:], T.SAME[:], Op.mult, ["tF", "SAME"], ["TRI"])
-    ts(T.VO[:], T.w0s[:], 8, None, Op.add, None, ["w0s"], ["VO0", "VO1"])
-    deferred = []
-
-    def later(f, *a):
-        deferred.append(lambda: f(*a))
-    later(cp, T.IH[:], T.IB[:], ["IB"], ["IH"])
-    later(ts, cf(8), ci(4), 2.0, -1.0, Op.mult, Op.add, ["KI4"], [kk(8)])
-    later(ts, cf(9), ci(4), -15.0, 15.0, Op.mult, Op.add, ["KI4"], [kk(9)])
-    later(ts, T.TR[:], T.cI[:, 0:16], 16, cf(6), Op.mult, Op.add, ["cI", kk(6)], ["TR"])
-    later(ts, cf(19), PM, 10.5, -1.0, Op.is_lt, Op.mult, [kk(1)], [kk(19)])
+    ts(T.SAME[:], T.cgI[:], PG, None, Op.is_equal, None, ["cgI", "PG"], ["SAME"])
+    for nm, f in (("B2", 2.0), ("BN", -1.0), ("BH", 1.0)):
+        ts(T[nm][:], c8, PG, f, Op.is_equal, Op.mult, ["cI", "PG"], [nm], 8)
+    tt(T.ZM1[:], T.tF[:], T.SAME[:], Op.mult, ["tF", "SAME"], ["ZM1"], 256)
+    lin(T.ZM0[:], T.ZM1[:], 1.0, 0.0, ["ZM1"], "ZM0")
+    lin(T.ZM0[:, 0::16], T.SAME[:, 0::16], 1.0, 0.0, ["SAME"], "ZM0", 8)
+    ts(T.DC[:], T.cmI[:], 15, 65.0, Op.is_equal, Op.add, ["cmI"], ["DC"])
+    col("s0", 14, -1.0, 1.0)
+    col("o0", 14, -1.0, 8.0)
+    col("s1", 14, -2.0, 1.0)
+    col("o1", 14, float(W + K), 8.0)
+    col("n14", 14, -1.0, 0.0)
+    col("ad", 14, 258.0, -2.0)
+    col("lo", 12, 1.0, -0.5)
+    col("lo", 15, 1.0, "lo")
+    col("hi", 13, 1000.0, 0.5)
+    col("hi", 15, 1.0, "hi")
+    col("nov", 11, -1.0, 1.0)
+    col("nov", 15, -1.0, "nov")
+    lin(cf("ct"), cf("low"), -0.5 + 2.0 ** -12, m16(12), ["low", "M16"], "ct", 1)
+    col("ct", 11, 8.5, "ct")
+    col("ct", 15, 9.5, "ct")
+    lin(cf("sc"), cf("low"), 1024 * U, 0.0, ["low"], "sc", 1)
+    col("sc", 11, 256 * U, "sc")
+    col("sc", 15, -256 * U, "sc")
+    col("bi", 12, -11 * 512 * U, 0.0)
+    col("bi", 13, -U, "bi")
+    col("bi", 11, 256 * U, "bi")
+    col("bi", 15, 256 * U, "bi")
+    lin(cf("i4"), cf("low"), 4095.0, 1.0, ["low"], "i4", 1)
+    lin(cf("h4"), cf("low"), -4096.0, 0.0, ["low"], "h4", 1)
+    fill(cf("yc"), -135.5, [], "yc", 1)
+    ts(ci(2), ci(0), -1, 30, Op.mult, Op.add, ["KI0"], ["KI2"], 1)
+    tt(cf("g16"), P0, PM, Op.subtract, ["P0", "PM"], ["g16"], 1)
+    ts(ci(3), ci(2), 15, None, Op.bitwise_and, None, ["KI2"], ["KI3"], 1)
+    ts(cf("sel"), PM, 14.5, -2048.0, Op.is_lt, Op.mult, ["PM"], ["sel"], 1)
+    tt(cf("perm"), ci(3), cf("g16"), Op.add, ["KI3", "g16"], ["perm"], 1)
+    cp(T.BLK[:], T.SAME[:], ["SAME"], ["BLK"])
+    ts(T.PERM[:], c128, cf("perm"), None, Op.is_equal, None, ["cI", "perm"], ["PERM"])
+    ts(T.MK[:], T.cmI[:], PM, None, Op.is_equal, None, ["cmI", "PM"], ["MK"])
+    ts(cf("tri"), m16(15), -1000.0, P0, Op.mult, Op.add, ["M16", "P0"], ["tri"], 1)
+    ts(T.tF[:], c128, cf("tri"), 1024.0, Op.is_le, Op.mult, ["cI", "tri"], ["tF"])
+    tt(T.TRI[:], T.tF[:], T.SAME[:], Op.mult, ["tF", "SAME"], ["TRI"], 256)
+    ts(T.VO[:], T.w0s[:], 8, None, Op.add, None, ["w0s"], ["VO0", "VO1"], 16)
     for j in range(11):
-        later(op, "V", lambda j=j: v.memset(T.PW[:, j::16], 2.0 ** -(j + 1)), ["PW"], ["PWx%d" % j])
-    later(tt, T.WB[:], T.PW[:], T.SAME[:], Op.mult, ["PW", "SAME"] + ["PWx%d" % j for j in range(11)], ["WB"])
-    later(ts, T.CT[:], T.cI[:], cf(13), cf(18), Op.mult, Op.add, ["cI", kk(13), kk(18)], ["CT"])
-    later(ts, T.WH[:], T.IB[:], cf(19), None, Op.mult, None, ["IB", kk(19)], ["WH"])
-    later(ts, T.tF[:], T.cmI[:], 11, -1.0, Op.is_equal, Op.mult, ["cmI"], ["tF"])
-    later(ts, cf(30), PM, 10.5, 2048.0, Op.is_lt, Op.mult, [kk(1)], [kk(30)])
-    later(cp, cf(26), ci(5), ["KI5"], [kk(26)])
-    later(ts, cf(27), ci(5), -1.0, 1.0, Op.mult, Op.add, ["KI5"], [kk(27)])
-    later(tt, T.WC[:], T.tF[:], T.SAME[:], Op.mult, ["tF", "SAME"], ["WC"])
-    for (base, par) in ((20, 27), (23, 26)):
-        later(ts, T.KF[:, base:base + 3], T.KF[:, 30:33], cf(par), None, Op.mult, None, [kk(30), kk(31), kk(32), kk(par)], [kk(base)])
+        fill(T.PW[:, j::16], 2.0 ** -(j + 1), ["PW"], "PWx%d" % j)
+    tt(T.WB[:], T.PW[:], T.SAME[:], Op.mult, ["PW", "SAME"] + ["PWx%d" % j for j in range(11)], ["WB"], 256)
+    ts(T.WB4[:], T.WB[:], 4096.0, None, Op.mult, None, ["WB"], ["WB4"], 64)
+    cp(T.IH[:], T.IB[:], ["IB"], ["IH"], 64)
+    ts(T.I4[:], T.IB[:], cf("i4"), None, Op.mult, None, ["IB", "i4"], ["I4"], 64)
+    ts(T.WH4[:], T.IB[:], cf("h4"), None, Op.mult, None, ["IB", "h4"], ["WH4"], 64)
+    ts(T.CT[:], c128, m16(13), cf("ct"), Op.mult, Op.add, ["cI", "M16", "ct"], ["CT"])
+    ts(cf("sg"), ci(4), -7.5, 8.5, Op.mult, Op.add, ["KI4"], ["sg"], 1)
+    lin(T.AD[:], T.cF[:], cf("n14"), cf("ad"), ["cF", "n14", "ad"], "AD", 256)
+    for nm, parts in (("WC", (slice(11, 128, 16), slice(15, 128, 16))), ("WS", (slice(0, 128, 2),))):
+        lin(T[nm][:], T.SAME[:], 0.0, 0.0, ["SAME"], nm)
+        for p in parts:
+            lin(T[nm][:, p], T.SAME[:, p], -1.0, 0.0, ["SAME"], nm, 32)
+    lin(T.I75[:], T.IB[:], 7.5, 0.0, ["IB"], "I75")
+    lin(T.C75[:], T.SAME[:], 0.0, 7.5, ["SAME"], "C75")
+    for p in PART.values():
+        lin(T.TR[:, p], T.cF[:, 0:8], 16.0, PM, ["cF", "PM"], "TR", 8)
+    lin(T.WI[:], T.TR[:, 0:8], U, 0.0, ["TR"], "WI", 8)
+    lin(T.CVS[:], T.WI[:], 0.0, float(GB), ["WI"], "CVS", 8)
+    lin(T.CVVS[:], T.WI[:], -1.0, float(GB), ["WI"], "CVVS", 8)
+    lin(T.CVVS[:, 1::2], T.WI[:, 1::2], 0.0, float(GB), ["WI"], "CVVS", 8)
+    for nm, c in (("SC", "sc"), ("BI", "bi")):
+        lin(T[nm][:], T.SAME[:, 0::16], cf(c), 0.0, ["SAME", c], nm, 8)
 
+    def hf(b): return rank // 4 if b else 1 - rank // 4
     def buf(n, b): return T[n + "%d" % b]
     def key(n, b): return "%s%d" % (n, b)
-    def xread(t): return ["X", "Xd"] + (["Xown0", "Xarr0"] if t else [])
-    def xwin(t): return T.X[:, GB:N0 + W + K * t]
+    def xread(t): return ["X", "Xd"] + (["Xe", "Xown0", "Xarr0"] if t else [])
+    def xwin(t): return T.X[:, GB:AC + 8] if t else T.X[:, GB:N0 + W]
     def awin(t): return T.A[:, GB:N0 + W + K * t]
-    def vo(b): return T.VO[:, 8 * b:8 * b + 8]
+    def vo(b): return T.VO[:, 8 * hf(b):8 * hf(b) + 8]
     def wb(b): return slice(128 * b, 128 * b + 128)
+    def dk(b, lo, hi): return ["D%d_%d" % (b, j) for j in range(lo // 8, hi // 8)]
 
-    def links(t, b):
-        op("V", lambda: v.tensor_scalar(buf("AO", b)[:], awin(t).indirect(vo(b)), 8, None, Op.add),
-           ["A", "Ad", "Anew0", "Anew1", key("VO", b)], [key("AO", b)])
-
-    def numbers(t, b, hs=(0, 1)):
-        for h in hs:
-            ac(buf("D", b)[:, 1024 * h:1024 * h + 1024], xwin(t).indirect(buf("AO", b)[:, 64 * h:64 * h + 64]), AF.Copy,
-               [key("AO", b)] + xread(t), ["D%d%d" % (b, h)])
+    def links(t, b, k):
+        new = t and k
+        ts(buf("AO", b)[:], awin(1 if new else 0).indirect(vo(b)), cf("s%d" % t), cf("o%d" % t), Op.mult, Op.add,
+           ["A", "Ad", key("VO", b), "s%d" % t, "o%d" % t] + (["Anew0", "Anew1"] if new else []), [key("AO", b)], 128 * GATHER)
 
     def half(b):
-        cp(buf("AH", b)[:], buf("AO", b)[:], [key("AO", b)], [key("AH", b)])
+        cp(buf("AH", b)[:], buf("AO", b)[:], [key("AO", b)], [key("AH", b)], 64)
+        mm(buf("ch", b)[:, 0:128], T.PERM[:], buf("AH", b)[:], True, False, ["PERM", key("AH", b)], key("ch", b))
 
-    def gather_y(t, b):
-        cp(T.Y[:, wb(b)], xwin(t).indirect(vo(b)), [key("VO", b)] + xread(t), [key("Y", b)])
+    def gather(q, t, o, lst, n, reads, writes):
+        if q == "S":
+            ac(o, xwin(t).indirect(lst), AF.Copy, reads + xread(t), writes, n * GATHER, bias=128.0)
+        else:
+            ts(o, xwin(t).indirect(lst), 128.0, None, Op.add, None, reads + xread(t), writes, n * GATHER)
+
+    def numbers(t, b, cuts):
+        for q, lo, hi in cuts:
+            if hi > lo:
+                gather(q, t, buf("D", b)[:, 16 * lo:16 * hi], buf("AO", b)[:, lo:hi], 16 * (hi - lo), [key("AO", b)], dk(b, lo, hi))
+
+    def add_y(t, b):
+        if "y" in "".join(PLAN):
+            return tt(buf("SY", b)[:], xwin(t).indirect(vo(b)), buf("Z", b)[:], Op.add, [key("VO", b), key("Z", b)] + xread(t), [key("SY", b)], 128 * GATHER)
+        gather("S", t, buf("Y", b)[:], vo(b), 128, [key("VO", b)], [key("Y", b)])
 
     def halve(b):
-        o = buf("ch", b)[:, 384:512]
-        mm(o, T.WR[:, 0:128], buf("Z", b)[:], True, False, ["WR", key("Z", b)], key("ch", b))
-        mm(o, T.WR[:, 0:128], T.Y[:, wb(b)], False, True, ["WR", key("Y", b)], key("ch", b))
+        for nm in "ZY":
+            mm(buf("dist", b)[:, 128:256], T.WR[:, 0:128], buf(nm, b)[:], nm == "Z", nm == "Y", ["WR", key(nm, b)], key("dist", b))
 
     def new_z(b):
-        ts(buf("Z", b)[:], buf("ch", b)[:, 384:512], MAGIC, MAGIC, Op.add, Op.subtract, [key("ch", b)], [key("Z", b)])
+        if "y" in "".join(PLAN):
+            return ts(buf("Z", b)[:], buf("SY", b)[:], 0.5, 63.8, Op.mult, Op.add, [key("SY", b)], [key("Z", b)], 64)
+        ts(buf("Z", b)[:], buf("dist", b)[:, 128:256], MAGIC, MAGIC - 2, Op.add, Op.subtract, [key("dist", b)], [key("Z", b)])
 
-    def spread_z(b):
-        for r in range(KZ):
-            mm(buf("zp", b)[:, r::KZ], T.IB[:], buf("Z", b)[:], True, True, ["IB", key("Z", b)], key("zp", b))
-        mm(buf("dist", b)[:, 0:128], buf("Z", b)[:], T.ZM[:], True, False, ["ZM", key("Z", b)], key("dist", b))
+    def spread(b, hs=(0, 1)):
+        for h in hs:
+            for r in range(max(16 // st for lo, hi, a, st in PIECES.values() if lo // 64 == h)):
+                mm(T["zp%d%d" % (b, h)][:, :, r], T.IB[:], buf("Z", b)[:, 64 * h:64 * h + 64], True, True, ["IB", key("Z", b)], "zp%d%d" % (b, h), 64)
 
-    def bar(b, k):
+    def bars(t, b, k):
+        kd = key("dist", b)
+        mm(T[kd][:, 0:128], buf("Z", b)[:], buf("ZM", t)[:], True, False, [key("ZM", t), key("Z", b)], kd)
         for k2 in range(k):
-            mm(buf("dist", b)[:, 0:128], buf("SA", b)[:, wb(k2)], T.TRI[:], False, False, ["TRI", key("SA", b)], key("dist", b))
+            mm(T[kd][:, 0:128], buf("SA", b)[:, wb(k2)], T.TRI[:], False, False, ["TRI", "SA%d%d" % (b, k2)], kd)
 
-    def sums_d(t, b):
-        for i in range(15):
-            w = T.B1 if (t == 0 and i == 14) else T.BN
-            mm(buf("dist", b)[:, 14 - i:128:16], buf("D", b)[:, i::16], w[:], False, False, ["B1", "BN", "D%d0" % b, "D%d1" % b], key("dist", b))
+    def maxima(t, b, p):
+        lo, hi, a, st = PIECES[p]
+        kz, r = "zp%d%d" % (b, lo // 64), slice(16 * lo + a, 16 * hi, st)
+        tt(buf("M", b)[:, r], buf("D", b)[:, r], T[kz][:, lo % 64:(hi - 1) % 64 + 1, 0:16 // st], Op.max,
+           dk(b, lo, hi) + [kz], ["M%d%d_%d" % (b, j, i) for j in range(lo // 16, hi // 16) for i in range(a, 16, st)], 16 * (hi - lo) // st)
 
-    PLAN = [[[(0, 4)], [(1, 4)], [(2, 8), (6, 16)], [(3, 8), (7, 16)]], [[(0, 4)], [(1, 4)], [(2, 4)], [(3, 8), (7, 16)]]]
+    def sums(t, b):
+        kd = key("dist", b)
+        for i in range(14 + t):
+            mm(T[kd][:, 14 - i:128:16], buf("D", b)[:, i::16], T.BN[:], False, False, ["BN"] + dk(b, 0, 128), kd, 64)
 
-    def max_op(t, b, h, j):
-        for (a, st) in PLAN[t][j]:
-            r = slice(1024 * h + a, 1024 * h + 1024, st)
-            tt(buf("M", b)[:, r], buf("D", b)[:, r], buf("zp", b)[:, 256 * h:256 * h + 256:st // 4], Op.max, ["D%d%d" % (b, h), key("zp", b)], ["M%d%d%d" % (b, h, a)])
+    def sums_m(t, b):
+        kd = key("dist", b)
+        order = sorted(range(14 + t), key=lambda i: i % 2)
+        for i in order:
+            mm(T[kd][:, 14 - i:128:16], buf("M", b)[:, i::16], T.B2[:], False, i == order[-1], ["B2"] + ["M%d%d_%d" % (b, j, i) for j in range(8)], kd, 64)
 
-    def sums_m(t, b, j):
-        for (a, st) in PLAN[t][j]:
-            for i in range(a, 16, st):
-                mm(buf("dist", b)[:, 14 - i:128:16], buf("M", b)[:, i::16], T.B2[:], False, i == 7,
-                   ["B2", "M%d0%d" % (b, a), "M%d1%d" % (b, a)], key("dist", b))
+    def select(b, k, gap):
+        ch, kc, nt, sa, ks = buf("ch", b), key("ch", b), buf("NT", b), buf("SA", b)[:, wb(k)], "SA%d%d" % (b, k)
+        op("V", lambda: v.tensor_tensor_scan(nt[:, 1:129], buf("dist", b)[:, 0:128], T.DC[:], 66.0, Op.min, Op.max), [key("dist", b), "DC"], [key("NT", b)])
+        mm(ch[:, 0:128], nt[:, 0:128], T.IP[:], False, False, ["IP", key("NTi", b), key("NT", b)], kc)
+        mm(ch[:, 0:128], nt[:, 1:129], T.IN[:], False, True, ["IN", key("NT", b)], kc)
+        gap(1)
+        ts(sa, ch[:, 0:128], cf("sel"), 0.0, Op.add, Op.max, [kc, "sel"], [ks])
+        mm(ch[:, 128:256], sa, T.BLK[:], True, True, ["BLK", ks], kc)
+        gap(2)
+        tt(buf("LT", b)[:], ch[:, 128:256], T.MK[:], Op.mult, [kc, "MK"], [key("LT", b)])
+        mm(ch[:, 256:264], buf("LT", b)[:], T.BH[:], True, True, ["BH", key("LT", b)], kc, 64)
+        gap(3)
+        cp(vo(b), ch[:, 256:264], [kc], [key("VO", b)], 8)
+        gap(4)
 
-    def sel_a(b):
-        ts(buf("NV", b)[:], buf("dist", b)[:, 0:128], 65.5, None, Op.is_ge, None, [key("dist", b)], [key("NV", b)])
-        op("V", lambda: v.tensor_tensor_scan(buf("NT", b)[:, 1:129], buf("NV", b)[:], T.DC[:], 1.0, Op.mult, Op.max), [key("NV", b), "DC"], [key("NT", b)])
-        o = buf("ch", b)[:, 0:128]
-        mm(o, T.PERM[:], buf("AH", b)[:], True, False, ["PERM", key("AH", b)], key("ch", b))
-        mm(o, buf("NT", b)[:, 0:128], T.IP[:], False, False, ["IP", key("NTi", b), key("NT", b)], key("ch", b))
-        mm(o, buf("NT", b)[:, 1:129], T.IN[:], False, True, ["IN", key("NT", b)], key("ch", b))
+    def lists(t, b):
+        o = buf("ch", b)[:, 256:264]
+        for p in "k" if t else "kl":
+            tt(buf("VF", b)[:, PART[p]], o, T["CV" + SUMS[p + str(b)]][:], Op.add, [key("ch", b), "CV" + SUMS[p + str(b)]], [key("VF" + p, b)], 8)
 
-    def sel_b(b, k):
-        sa = buf("SA", b)[:, wb(k)]
-        ts(sa, buf("ch", b)[:, 0:128], cf(4), 0.0, Op.add, Op.max, [key("ch", b), kk(4)], [key("SA", b)])
-        mm(buf("ch", b)[:, 128:256], sa, T.BLK[:], True, True, ["BLK", key("SA", b)], key("ch", b))
+    def bits(t, b):
+        kd, sa, ks = key("dist", b), buf("SA", b)[:, wb(S - 1)], "SA%d%d" % (b, S - 1)
+        mm(T[kd][:, 128:256], T.IH[:], T.CT[:], True, False, ["IH", "CT"], kd)
+        mm(T[kd][:, 128:256], T.WB[:], sa, False, True, ["WB", ks], kd)
+        ts(buf("HH", b)[:], T[kd][:, 128:256], MAGIC, MAGIC, Op.add, Op.subtract, [kd], [key("HH", b)])
+        mm(T[kd][:, 256:384], T.I4[:], T.CT[:], True, False, ["I4", "CT"], kd)
+        mm(T[kd][:, 256:384], T.WB4[:], sa, False, False, ["WB4", ks], kd)
+        mm(T[kd][:, 256:384], T.WH4[:], buf("HH", b)[:], False, False, ["WH4", key("HH", b)], kd)
 
-    def sel_c(b):
-        tt(buf("LT", b)[:], buf("ch", b)[:, 128:256], T.MK[:], Op.mult, [key("ch", b), "MK"], [key("LT", b)])
-        mm(buf("ch", b)[:, 256:264], buf("LT", b)[:], T.BH[:], True, True, ["BH", key("LT", b)], key("ch", b))
+    def vote(t, b):
+        kd = key("dist", b)
+        gather("S", t, buf("Y", b)[:], vo(b), 128, [key("VO", b)], [key("Y", b)])
+        lin(buf("SY", b)[:], buf("Z", b)[:], 1.0, -128.0, [key("Z", b)], key("SY", b))
+        tt(buf("GT", b)[:], xwin(t).indirect(vo(b)), buf("SY", b)[:], Op.is_gt, [key("VO", b), key("SY", b)] + xread(t), [key("GT", b)], 128 * GATHER)
+        mm(T[kd][:, 256:384], T.WC[:], buf("GT", b)[:], False, True, ["WC", key("GT", b)], kd)
 
-    def sel_d(b):
-        cp(vo(b), buf("ch", b)[:, 256:264], [key("ch", b)], [key("VO", b)])
+    def rows(t, b):
+        kd = key("dist", b)
+        ts(buf("Rk", b)[:], T[kd][:, 256:384], cf("lo"), cf("hi"), Op.max, Op.min, [kd, "lo", "hi"], [key("Rk", b)])
+        if t == 0:
+            lin(buf("Rl", b)[:], buf("Rk", b)[:], cf("nov"), 0.0, [key("Rk", b), "nov"], key("Rl", b))
 
-    def bits1(b):
-        for lo in (128, 256):
-            o = buf("dist", b)[:, lo:lo + 128]
-            mm(o, T.IH[:], T.CT[:, wb(b)], True, False, ["IH", "CT"], key("dist", b))
-            mm(o, T.WB[:], buf("SA", b)[:, wb(4)], False, lo == 128, ["WB", key("SA", b)], key("dist", b))
-
-    def bits2(b):
-        ts(buf("HH", b)[:], buf("dist", b)[:, 128:256], MAGIC, MAGIC, Op.add, Op.subtract, [key("dist", b)], [key("HH", b)])
-
-    def vote(b):
-        tt(T.GT[:, wb(b)], T.Y[:, wb(b)], buf("zp", b)[:, 0::KZ], Op.is_gt, [key("Y", b), key("zp", b)], [key("GT", b)])
-        o = buf("dist", b)[:, 256:384]
-        mm(o, T.WH[:], buf("HH", b)[:], False, False, ["WH", key("HH", b)], key("dist", b))
-        mm(o, T.WC[:], T.GT[:, wb(b)], False, True, ["WC", key("GT", b)], key("dist", b))
-
-    def bits3(b):
-        ts(T.RB[:, wb(b)], buf("dist", b)[:, 256:384], 0.0, 0.5, Op.is_gt, Op.subtract, [key("dist", b)], [key("RB", b)])
-
-    def left(b, q):
-        for (nm, base) in (("LE", 20), ("LO", 23)):
-            if q == "V":
-                ts(T[nm][:, wb(b)], T.RB[:, wb(b)], cf(base), cf(base + 1 + b), Op.mult, Op.add, [key("RB", b), kk(base)], [key(nm, b)])
+    def firsts(t, b, banks):
+        kds = ["BD%d%d" % (b, gg) for gg in range(8)]
+        for gg in range(8):
+            o, r, s1, s2 = buf("BD", b)[:, :, 16 * gg:16 * gg + 16], buf("Rk", b)[:], T.SC[:, gg:gg + 1], T.BI[:, gg:gg + 1]
+            if DIAG[b][gg] == "V":
+                ts(o, r, s1, s2, Op.mult, Op.add, [key("Rk", b), "SC", "BI"], [kds[gg]], 64)
             else:
-                ac(T[nm][:, wb(b)], T.RB[:, wb(b)], AF.Identity, [key("RB", b), kk(base)], [key(nm, b)], scale=cf(base), bias=cf(base + 1 + b))
+                ac(o, r, AF.Identity, [key("Rk", b), "SC", "BI"], [kds[gg]], scale=s1, bias=s2)
+        kas = []
+        for p, bks in banks:
+            def part(a):
+                n, kb, lo = 16 * a + 16 if p == "l" else 128, bks[a % 2], 128 * (a // 2)
+                return n, kb, T[kb][:, lo // 8:(lo + n) // 8, :] if kb[0] == "z" else T[kb][:, lo:lo + n]
+            for a in range(8):
+                n, kb, src = part(a)
+                mm(src, buf("BD", b)[:, a, :], buf("R" + p, b)[:, 0:n], True, True, [key("R" + p, b)] + kds, kb, max(n, 64))
+            for a in range(8):
+                n, kb, src = part(a)
+                acc, ka = buf("AC", b)[:, PART[p].start + a:PART[p].start + a + 1], "AC%s%d%d" % (p, b, a)
+                kas.append(ka)
+                if SUMS[p + str(b)] == "VS" and a % 2 == 0:
+                    op("V", lambda acc=acc, src=src: v.tensor_reduce(acc, src, AxisListType.X, Op.max), [kb], [ka], cost=n)
+                else:
+                    ac(T.junk[:, 128 * (a % 4):128 * (a % 4) + n], src, AF.Relu, [kb, "WI"], [ka, "junk%d" % (a % 4)], n + 24, bias=T.WI[:, a:a + 1], accum_out=acc)
+        n = 8 * len(banks)
+        ff, kf = buf("FF", b)[:, 0:n], key("FF", b)
+        tt(ff, buf("VF", b)[:, 0:n], buf("AC", b)[:, 0:n], Op.subtract, [key("VF" + p, b) for p, _ in banks] + kas, [kf], 16)
+        tt(ff, ff, T.TR[:, 0:n], Op.max, [kf, "TR"], [kf], 16)
+        cp(buf("OF", b)[:, 0:n], ff, [kf], [key("OF", b)], 8)
 
-    def flipped(b):
-        ac(T.FY[:, wb(b)], T.Y[:, wb(b)], AF.Identity, [key("Y", b), kk(8), kk(9)], [key("FY", b)], scale=cf(8), bias=cf(9))
+    def flip(t, b):
+        o, kd, f = buf("dist", b)[:, 128:256], key("dist", b), buf("F", t)
+        mm(o, T.WS[:], buf("GT", b)[:], True, True, ["WS", key("GT", b)], kd)
+        ac(buf("SG", b)[:], o, AF.Sign, [kd, "sg"], [key("SG", b)], bias=cf("sg"))
+        win, wk = T.X[:, 0:N0 + W + K * t].indirect(buf("OF", b)[:, 0:8]), [key("OF", b), "Xd"] + (["Xown0", "Xarr0"] if t else [])
+        if b == 0:
+            cp(f[:, 0:N0 + W + K * t].indirect(T.OF0[:, 0:8]), T.SG0[:], ["OF0", "SG0"], [key("F", t)], 128 * SCATTER)
+            mm(o, T.IB[:], T.Y0[:], True, False, ["IB", "Y0"], kd)
+            mm(o, T.I75[:], T.SG0[:], False, True, ["I75", "SG0"], kd)
+            ac(T.TV0[:], o, AF.Abs, [kd, "yc"], ["TV0"], bias=cf("yc"))
+            cp(win, T.TV0[:], wk + ["TV0"], ["X"], 128 * SCATTER)
+        else:
+            lin(T.YC[:], T.Y1[:], 1.0, -135.5, ["Y1"], "YC")
+            tt(T.FG[:], f[:, GB:N0 + W + K * t].indirect(vo(1)), T.SG1[:], Op.max, [key("F", t), "VO1", "SG1"], ["FG"], 128 * GATHER)
+            tt(T.TV1[:], T.FG[:], T.YC[:], Op.mult, ["FG", "YC"], ["TV1"], 256)
+            tt(win, T.TV1[:], T.C75[:], Op.add, wk + ["TV1", "C75"], ["X"], 128 * SCATTER)
 
-    def turn(b):
-        for j in range(4):
-            d = (4 * b + j - rank) % 8
-            rot = T.WR[:, 128 - 16 * d:256 - 16 * d]
-            oo = buf("ch", b)[:, 384 + 32 * j:416 + 32 * j]
-            mm(oo, rot, buf("Z", b)[:, 32 * j:32 * j + 32], True, False, ["WR", key("Z", b)], key("ch", b))
-            mm(oo, rot, T.Y[:, 128 * b + 32 * j:128 * b + 32 * j + 32], False, True, ["WR", key("Y", b)], key("ch", b))
-
-    sent = [0]
+    def new_links(b):
+        c = N0 + W + 128 * hf(b)
+        tt(buf("VAL", b)[:], awin(0).indirect(vo(b)), T.AD[:, wb(hf(b))], Op.max, ["A", "Ad", key("VO", b), "AD"], [key("VAL", b)], 128 * GATHER)
+        dma("Y", T.A[15::16, c:c + 128], buf("VAL", b)[15::16, :], key("suc", b), 16, [key("VAL", b), "Af"], [key("Anew", b)])
+        cp(T.A[:, 0:N0 + W].indirect(buf("OF", b)[:, 8:16]), buf("VAL", b)[:], [key("OF", b), key("VAL", b), "Ad"], ["A"], 128 * SCATTER)
 
     def send(t, b):
-        zs, o = T["ZS%d" % t], buf("ch", b)
-        c0 = N0 + W + K * t + 32 * rank
-        ts(zs[:, wb(b)], o[:, 384:512], MAGIC, MAGIC, Op.add, Op.subtract, [key("ch", b)], ["ZS%d%d" % (t, b)])
-        if rank // 4 == b:
-            j = rank % 4
-            ts(T.X[:, c0:c0 + 32], o[:, 384 + 32 * j:416 + 32 * j], MAGIC, MAGIC, Op.add, Op.subtract, [key("ch", b)], ["Xown%d" % t])
-        deps("G", ["ZS%d%d" % (t, b)], [])
+        zs, o, h, kz = T["ZS%d" % t], buf("ch", b), hf(b), "ZS%d%d" % (t, b)
+        for j in range(4):
+            d = (4 * h + j - rank) % 8
+            rot = T.WR[:, 128 - 16 * d:256 - 16 * d]
+            mm(o[:, 384 + 32 * j:416 + 32 * j], rot, buf("Z", b)[:, 32 * j:32 * j + 32], True, False, ["WR", key("Z", b)], key("ch", b), 64)
+            mm(o[:, 384 + 32 * j:416 + 32 * j], rot, buf("Y", b)[:, 32 * j:32 * j + 32], False, True, ["WR", key("Y", b)], key("ch", b), 64)
+        c0 = N0 + W + 32 * rank
+        land = T.XA[:, 32 * rank:32 * rank + 32] if t else T.X[:, c0:c0 + 32]
+        if b:
+            ts(zs[:, wb(h)], o[:, 384:512], MAGIC, MAGIC + 126, Op.add, Op.subtract, [key("ch", b)], [kz])
+        else:
+            lin(T.ZT[:], o[:, 384:512], 1.0, 2.0, [key("ch", b)], "ZT")
+            lin(zs[:, wb(h)], T.ZT[:], 1.0, -128.0, ["ZT"], kz)
         trs, used = [], set()
-        for q in sorted([q for q in range(4 * b, 4 * b + 4) if q != rank], key=lambda q: len(topo.engines(core, T.cores[q]))):
+        for q in range(4 * h, 4 * h + 4):
+            if q == rank:
+                continue
             dst = T.cores[q]
-            es = topo.engines(core, dst)
-            es = es[0::2] + es[1::2]
-            if dst in topo.cores_of(core):
-                es = es[::-1]
-            e = [x for x in es if x not in used][0]
-            used.add(e)
+            es = [x for x in topo.engines(core, dst) if x not in used]
+            es = es[-ENG[b]:] if dst in topo.cores_of(core) else es[:ENG[b]]
+            used.update(es)
             rid, pid = topo.addr(dst, core)
-            trs.append(RemoteDMATransfer(dst_ids=[DstId(rid=rid, pnc=pid)], dma_engine_mask=1 << e, remote_sem=sem["arr%d" % t],
-                                         src=zs[:, 32 * q:32 * q + 32], dst=T.X[:, c0:c0 + 32]))
-        g.remote_dma_fused(trs, local_sem=sem["snt"])
-        sent[0] += len(trs)
-
-    def pairs(bk, lo, gg, c, first, last, kb):
-        a, nm = gg // 2, "LE" if gg % 2 == 0 else "LO"
-        tri = first <= 128 * c < last
-        mm(bk[:, lo:lo + last - first], T[nm][32 * a:32 * a + 32, wb(c)], T.RB[32 * a:32 * a + 32, first:last], True, not tri,
-           [key(nm, c), "RB0"] + (["RB1"] if last > 128 else []), kb)
-        if tri:
-            mm(bk[:, lo + 128 * c - first:lo + 128 * c - first + 128], T.IB[:], T.T2[:], False, True, ["IB", "T2"], kb)
-
-    def reduce_v(src, j, kb):
-        op("V", lambda: v.tensor_reduce(T.ACV[:, j:j + 1], src, AxisListType.X, Op.max), [kb], ["ACV%d" % j])
-
-    def reduce_s(src, n, j, kb):
-        o = 256 * (j % 4)
-        ac(T.junk[:, o:o + n], src, AF.Relu, [kb], ["ACS%d" % j, "junk%d" % (j % 4)], accum_out=T.ACS[:, j:j + 1])
-
-    def place_v(nm, gg, j, an):
-        ts(T[nm][:, 16 * gg:16 * gg + 16], T.M5[:], T[an][:, j:j + 1], 0.0, Op.min, Op.max, ["M5", "%s%d" % (an, j)], ["%s%d" % (nm, gg)])
-
-    def place_s(nm, gg, j):
-        ac(T[nm][:, 16 * gg:16 * gg + 16], T.MN[:], AF.Relu, ["MN", "ACS%d" % j], ["%s%d" % (nm, gg)], bias=T.ACS[:, j:j + 1])
-
-    def early(gs):
-        kbs = ["eA", "eB", "dist0", "zp0"]
-        for gg in gs:
-            pairs(T[kbs[gg // 2]], 128 * (gg % 2), gg, 0, 0, 128, kbs[gg // 2])
-        for gg in gs:
-            reduce_s(T[kbs[gg // 2]][:, 128 * (gg % 2):128 * (gg % 2) + 128], 128, gg, kbs[gg // 2])
-
-    def new_links(t, b):
-        op("V", lambda: v.tensor_tensor(T.VAL[:, wb(b)], awin(t).indirect(vo(b)), T.AD[:, wb(b)], Op.max), ["A", "Ad", key("VO", b), "AD"], [key("VAL", b)])
-        ts(T.A[:, N0 + W + 128 * b:N0 + W + 128 * b + 128], T.VAL[:, wb(b)], m16(15), cf(11), Op.mult, Op.add, [key("VAL", b), "M16", kk(11)], [key("Anew", b)])
+            trs.append(RemoteDMATransfer(dst_ids=[DstId(rid=rid, pnc=pid)], dma_engine_mask=sum(1 << e for e in es), remote_sem=sem["arr%d" % t],
+                                         src=zs[:, 32 * q:32 * q + 32], dst=land))
+        op("G", lambda: g.remote_dma_fused(trs, local_sem=sem["snt"]), [kz], ["sent%d%d" % (t, b)], cost=200, lat=1.6 * DMA, tok=[])
+        if b:
+            lin(land, zs[:, 32 * rank:32 * rank + 32], 1.0, 0.0, [kz], "Xown%d" % t, 32)
+            op("", None, ["sent%d0" % t, "sent%d1" % t], ["Xarr%d" % t], cost=0, lat=0, tok=[("arr%d" % t, ARR)])
 
     def final_nodes(b):
-        mm(buf("ch", b)[:, 128:256], T.BLK[:], buf("SA", b)[:, wb(4)], True, True, ["BLK", key("SA", b)], key("ch", b))
-        ts(T.YV[:, wb(b)], buf("ch", b)[:, 128:256], 8.0, None, Op.subtract, None, [key("ch", b)], [key("YV", b)])
-
-    def late(t):
-        banks = [("eA", T.eA), ("eB", T.eB), ("dist0", T.dist0), ("dist1", T.dist1)]
-        for p in range(4):
-            for gg in (2 * p, 2 * p + 1):
-                kb, bk = banks[gg % 4]
-                pairs(bk, 0, gg, 0, 128, 256, kb)
-                pairs(bk, 256, gg, 1, 0, 256, kb)
-            if t and p < 2:
-                final_nodes(p)
-            for gg in (2 * p, 2 * p + 1):
-                kb, bk = banks[gg % 4]
-                if gg in (1, 3, 4, 6):
-                    reduce_s(bk[:, 0:128], 128, 8 + 2 * gg, kb)
-                    reduce_s(bk[:, 256:512], 256, 9 + 2 * gg, kb)
-                    place_s("LAB", gg, 8 + 2 * gg)
-                    place_s("LBB", gg, 9 + 2 * gg)
-                else:
-                    reduce_v(bk[:, 0:128], 2 * gg, kb)
-                    reduce_v(bk[:, 256:512], 2 * gg + 1, kb)
-                    place_v("LAB", gg, 2 * gg, "ACV")
-                    place_v("LBB", gg, 2 * gg + 1, "ACV")
-        ra, rb, rc = [["%s%d" % (nm, gg) for gg in range(8)] for nm in ("LAA", "LAB", "LBB")]
-        for (lo, w, wn) in (((256, T.B1, "B1"),) if t == 0 else ()) + ((288, T.B4, "B4"),):
-            oa, ob = T.ch0[:, lo:lo + 8], T.ch0[:, lo + 8:lo + 16]
-            isx = wn == "B4"
-            if isx:
-                mm(oa, T.LT0[:], T.BH[:], True, False, ["BH", "LT0"], "ch0")
-            mm(oa, T.LAA[:], w[:], not isx, False, [wn] + ra, "ch0")
-            mm(oa, T.LAB[:], w[:], False, True, [wn] + rb, "ch0")
-            if isx:
-                mm(ob, T.LT1[:], T.BH[:], True, False, ["BH", "LT1"], "ch0")
-            mm(ob, T.LBB[:], w[:], not isx, True, [wn] + rc, "ch0")
-        if t == 0:
-            ts(T.FR[:], T.ch0[:, 256:272], 511.5, -4096.0, Op.is_ge, Op.mult, ["ch0"], ["FR"])
-        tt(T.FF[:], T.ch0[:, 288:304], T.TR[:], Op.max, ["ch0", "TR"], ["FF"])
-        if t == 0:
-            tt(T.FR[:], T.FR[:], T.DV[:], Op.add, ["FR", "DV"], ["FR"])
-        ts(T.OFX[:], T.FF[:], float(GB), None, Op.add, None, ["FF"], ["OFX"])
-        if t == 0:
-            tt(T.FR[:], T.FR[:], T.TR[:], Op.max, ["FR", "TR"], ["FR"])
-            ts(T.OFA[:], T.FR[:], float(GB), None, Op.add, None, ["FR"], ["OFA"])
-            cp(T.A[:, 0:N0 + W].indirect(T.OFA[:]), T.VAL[:], ["OFA", "VAL0", "VAL1", "Ad"], ["A"])
-
-    def flip(t):
-        cp(T.X[:, 0:N0 + W + K * t].indirect(T.OFX[:]), T.FY[:], ["OFX", "FY0", "FY1", "Xd"] + (["Xown0", "Xarr0"] if t else []), ["X"])
+        mm(buf("ch", b)[:, 128:256], T.BLK[:], buf("SA", b)[:, wb(S - 1)], True, True, ["BLK", "SA%d%d" % (b, S - 1)], key("ch", b))
+        lin(T.YV[:, wb(hf(b))], buf("ch", b)[:, 128:256], 1.0, -8.0, [key("ch", b)], key("YV", b))
 
     for t in range(RO):
-        lastw["Xarr%d" % t] = [("arr%d" % t, 7)]
-        links(t, 0)
         if t:
-            flip(0)
-        numbers(t, 0, (1,))
-        links(t, 1)
-        numbers(t, 1)
+            dma("Y", T.yx[1::2, 0:W + K], T.X[1::2, N0:AC], "out4", 16, ["X", "Xown0", "Xarr0"], [])
         for b in range(2):
-            cp(buf("Z", b)[:], xwin(t).indirect(vo(b)), [key("VO", b)] + xread(t), [key("Z", b)])
-            spread_z(b)
-            if b == 0:
-                cp(T.D0[:, 0:1024], xwin(t).indirect(T.AO0[:, 0:64]), ["AO0"] + xread(t), ["D00"])
-        half(0)
-        half(1)
-        for j in range(4):
-            max_op(t, 0, 0, j)
-        pend = None
-        for k in range(S):
-            for b in range(2):
-                last = (b, k) == (1, S - 1)
-                nb = 1 - b
+            links(t, b, 0)
+            gather("V", t, buf("Z", b)[:], vo(b), 128, [key("VO", b)], [key("Z", b)])
+            numbers(t, b, [("V", 0, FILL[b]), ("S", FILL[b], max(FILL[b], 64)), ("S", max(FILL[b], 64), 128)])
+            spread(b)
+            bars(t, b, 0)
+            half(b)
+        for p in PIECES:
+            if p not in PLAN[0]:
+                maxima(t, 0, p)
+        for s in range(2 * S):
+            k, b = s // 2, s % 2
+            nb, nk = 1 - b, (s + 1) // 2
+            last = s == 2 * S - 1
 
-                def fill(*js):
-                    for j in js:
-                        if not last:
-                            max_op(t, nb, 0, j)
-                sums_d(t, b)
-                if last:
-                    bits2(0)
-                for j in range(4):
-                    max_op(t, b, 1, j)
-                    sums_m(t, b, j)
-                if pend:
-                    gather_y(t, nb)
-                    halve(nb)
-                    half(nb)
-                sel_a(b)
-                if pend:
-                    new_z(nb)
-                    spread_z(nb)
-                if last:
-                    vote(0)
-                for f in deferred[:4]:
-                    f()
-                del deferred[:4]
-                sel_b(b, k)
-                if last:
-                    turn(0)
-                    bits1(1)
-                    bits3(0)
-                    left(0, "S")
-                    flipped(0)
-                    if t == 0:
-                        new_links(t, 0)
-                fill(0)
-                sel_c(b)
-                if last:
-                    send(t, 0)
-                    bits2(1)
-                    early(range(0, 4))
-                fill(1, 2)
-                if pend:
-                    bar(*pend)
-                pend = None
-                sel_d(b)
-                if k < S - 1:
-                    links(t, b)
-                    numbers(t, b)
-                    pend = (b, k + 1)
-                    fill(3)
-                elif b == 0:
-                    bits1(0)
-                    ac(T.Y[:, wb(0)], xwin(t).indirect(vo(0)), AF.Copy, ["VO0"] + xread(t), ["Y0"])
-                    fill(3)
-                else:
-                    gather_y(t, 1)
-                    vote(1)
-                    bits3(1)
-                    left(1, "V")
-                    early(range(4, 8))
-                    turn(1)
-                    flipped(1)
-                    if t == 0:
-                        ts(T.DV[:], T.VO[:], 1.0, None, Op.mult, None, ["VO0", "VO1"], ["DV"])
-                    send(t, 1)
-                    if t == 0:
-                        new_links(t, 1)
-                    for gg in range(8):
-                        place_v("LAA", gg, gg, "ACS")
-                    late(t)
-    flip(RO - 1)
-    deps("S", ["X", "Xd", "Xown0", "Xarr0"], [])
-    act.dma_start(T.yx[:, 0:W + K], T.X[:, N0:N0 + W + K]).then_inc(sem.out2, 16)
-    deps("Y", ["YV0", "YV1"], [])
-    g.sync.dma_start(T.yv[:], T.YV[0::16, :]).then_inc(sem.out1, 16)
-    deps("Y", ["Xown1", "Xarr1"], [])
-    g.sync.dma_start(T.yx[:, W + K:W + 2 * K], T.X[:, N0 + W + K:N0 + W + 2 * K]).then_inc(sem.out3, 16)
-    for s, n in (("qV", cnt["V"]), ("qP", cnt["P"]), ("qS", cnt["S"]), ("qG", cnt["G"]), ("snt", sent[0]), ("arr0", 7), ("arr1", 7),
-                 ("out1", 16), ("out2", 16), ("out3", 16), ("ldw", 16), ("ldx", 16), ("ldal", 64), ("ldas", 64), ("ldn", 16)):
+            def gap(j):
+                if k == S - 1 and j == 2:
+                    bits(t, b)
+                if k == S - 1 and j == 4:
+                    vote(t, b)
+                for what in PLAN[j]:
+                    if what in PIECES:
+                        if j == 0 or not last:
+                            maxima(t, nb if j else b, what)
+                    elif 0 < s and not last:
+                        {"y": lambda: add_y(t, nb), "z": lambda: new_z(nb), "h": lambda: half(nb), "v": lambda: numbers(t, nb, [("V", 0, VS)]),
+                         "0": lambda: spread(nb, (0,)), "1": lambda: spread(nb, (1,)), "b": lambda: bars(t, nb, nk)}[what]()
+            chain["on"] = True
+            if last:
+                rows(t, 0)
+            sums(t, b)
+            if 0 < s and not last and "y" not in "".join(PLAN):
+                halve(nb)
+            gap(0)
+            sums_m(t, b)
+            if 0 < s and not last:
+                spread(nb, (0,))
+            chain["on"] = not last
+            select(b, k, gap)
+            if k < S - 1:
+                links(t, b, k + 1)
+                if "y" not in "".join(PLAN):
+                    add_y(t, b)
+                numbers(t, b, [("S", lo, hi) for lo, hi in zip((VS,) + SCUT, SCUT + (128,))])
+            gap(5)
+        rows(t, 1)
+        for b in range(2):
+            lists(t, b)
+            send(t, b)
+        for b in range(2):
+            firsts(t, b, [("k", ["ch0", "zp11" if b else "zp01"])] + [("l", ["ch1" if b else "ch0", "zp10" if b else "zp00"])] * (1 - t))
+            if t == 0:
+                new_links(b)
+            else:
+                final_nodes(b)
+            flip(t, b)
+    dma("S", T.yx[0::2, 0:W + K], T.X[0::2, N0:AC], "out2", 16, ["X"], [], 2 * DMA)
+    dma("Y", T.yv[:], T.YV[0::16, :], "out1", 16, ["YV0", "YV1"], [])
+    dma("Y", T.yx[:, W + K:W + 2 * K], T.XA[:], "out3", 16, ["Xown1", "Xarr1"], [])
+
+    clock = {q: {} for q in eng}
+    cnt = {q: 0 for q in "VPSG"}
+    snap = {}
+    for i in lay_out(calls):
+        c = calls[i]
+        q = c["q"]
+        if c["f"] is None:
+            continue
+        want = {}
+        for j, waits in c["before"].items():
+            for s, n in calls[j]["tok"] if waits else ():
+                want[s] = max(want.get(s, 0), n)
+        for s, n in want.items():
+            if clock[q].get(s, 0) < n:
+                eng[q].wait_ge(sem[s], n)
+                for s2, n2 in list(snap.get((s, n), {}).items()) + [(s, n)]:
+                    clock[q][s2] = max(clock[q].get(s2, 0), n2)
+        ins = c["f"]()
+        if c["tok"] is None:
+            ins.then_inc(sem["q" + q], 1)
+            cnt[q] += 1
+            c["tok"] = [("q" + q, cnt[q])]
+            snap[c["tok"][0]] = dict(clock[q])
+    for s, n in [("q" + q, cnt[q]) for q in cnt] + [("snt", RO * ARR), ("arr0", ARR), ("arr1", ARR), ("ldal", 48)] + \
+            [(s, 16) for s in ("out1", "out2", "out3", "out4", "suc0", "suc1", "ldw", "ldx", "ldas", "ldn")]:
         g.wait_ge(sem[s], n)

@@ -13,15 +13,17 @@ FILL = (48, 0)
 SCUT = (64, 96)
 PIECES = {"A": (0, 64, 0, 4), "B": (0, 64, 1, 4), "C": (0, 64, 2, 4), "D": (0, 64, 3, 4),
           "E": (64, 96, 0, 2), "F": (64, 96, 1, 2), "G": (96, 128, 0, 2), "H": (96, 128, 1, 2)}
-PLAN = ("GHzv", "1AB", "bC", "Dh", "E", "F")
+COPIES = (4, 8)
+PLAN = ("GHzv", "1AB", "bCDE", "", "h", "F")
 ENG = (2, 4)
 ARR = 4 * ENG[0] + 3 * ENG[1]
 DIAG = ("SVSSVSSV", "VVSVVSVV")
-SUMS = {"l0": "S", "k0": "VS", "l1": "S", "k1": "VS"}
+SUMS = {"l0": "VS", "k0": "VS", "l1": "S", "k1": "VS"}
 PART = {"k": slice(0, 8), "l": slice(8, 16)}
 FIX = {"V": 40, "S": 50, "P": 0, "G": 180, "Y": 100}
 GATHER, SCATTER, HOP, DMA, PE = 1.56, 3.8, 160, 2500, 0.6
 PASSES = 4
+EC = 1
 
 SCRATCH = {}
 
@@ -32,17 +34,16 @@ def declare(where, dtype, names, shape):
 
 
 declare("sbuf", "bfloat16", "X", [128, AC + 8])
-declare("sbuf", "bfloat16", "F0 F1", [128, AC])
 declare("sbuf", "int32", "A", [128, AC])
 declare("sbuf", "int32", "w0s KI", [128, 16])
 declare("sbuf", "uint16", "VO OF0 OF1", [128, 16])
-declare("sbuf", "bfloat16", "XA ZS0 ZS1 ZERO WR", [128, 256])
-declare("sbuf", "bfloat16", "junk", [128, 512])
+declare("sbuf", "bfloat16", "XA ZS0 ZS1 ZERO WR Rk0 Rk1", [128, 256])
+declare("sbuf", "bfloat16", "junk", [128, 1024])
 declare("sbuf", "float32", "YV AD cF", [128, 256])
 declare("sbuf", "float32", "M16 TR AC0 AC1 FF0 FF1 VF0 VF1", [128, 16])
 declare("sbuf", "float32", "WI CVS CVVS SC BI", [128, 8])
 declare("sbuf", "float32", "KF", [128, 40])
-declare("sbuf", "bfloat16", "IB IP IN ZM0 ZM1 MK DC WC WS I75 C75 Z0 Z1 SY0 SY1 Y0 Y1 YC GT0 GT1 Rl0 Rl1 Rk0 Rk1 SG0 SG1 FG TV0 TV1 ZT", [128, 128])
+declare("sbuf", "bfloat16", "IB IP IN ZM0 ZM1 MK DC WC WS I75 Z0 Z1 SY0 SY1 Y0 Y1 GT0 GT1 Rl0 Rl1 SG0 SG1 TV0 TV1 ZT", [128, 128])
 declare("sbuf", "bfloat16", "BD0 BD1", [128, 8, 128])
 declare("sbuf", "float16", "IH I4 TRI PERM BLK WB WB4 WH4 CT AH0 AH1 LT0 LT1 HH0 HH1", [128, 128])
 declare("sbuf", "float32", "tF SAME PW", [128, 128])
@@ -50,13 +51,12 @@ declare("sbuf", "int32", "cI cmI cgI VAL0 VAL1", [128, 128])
 declare("sbuf", "int32", "pI", [128, 1])
 declare("sbuf", "bfloat16", "B2 BN", [128, 8])
 declare("sbuf", "float16", "BH", [128, 8])
-declare("sbuf", "bfloat16", "D0 D1 M0 M1", [128, 2048])
+declare("sbuf", "bfloat16", "D0 D1 M0 M1 EC", [128, 2048])
 declare("sbuf", "uint16", "AO0 AO1", [128, 128])
 declare("sbuf", "bfloat16", "NT0 NT1", [128, 136])
 declare("sbuf", "float16", "SA0 SA1", [128, S * 128])
 BANKS = "dist0 dist1 ch0 ch1 zp00 zp01 zp10 zp11".split()
-declare("psum", "float32", "dist0 dist1 ch0 ch1", [128, 512])
-declare("psum", "float32", "zp00 zp01 zp10 zp11", [128, 64, 8])
+declare("psum", "float32", " ".join(BANKS), [128, 512])
 SEMAPHORES = ["qV", "qP", "qS", "qG", "ldw", "ldx", "ldal", "ldas", "ldn", "arr0", "arr1", "snt", "out1", "out2", "out3", "out4", "suc0", "suc1"]
 
 
@@ -178,14 +178,14 @@ def rank_program(g, core, T, topo):
     stripe("WR", 256, 63.0 / 128, 0)
     stripe("WR", 256, 63.0 / 128, 128, True)
     op("G", lambda: g.iota(T.A[:, N0 + W:AC], [[0, K]], -1, 0), ["WR"], ["Af"], cost=2 * K)
-    for t in range(RO):
-        op("G", lambda t=t: g.iota(T["F%d" % t][:, GB:AC], [[0, AC - GB]], -1, 0, allow_small_or_imprecise_dtypes=True), ["WR"], ["F%d" % t], cost=2 * AC)
     fill(T.X[:, GB:N0], 127.0, [], "Xd")
     fill(T.X[:, AC:AC + 8], 127.0, [], "Xe")
     fill(T.A[:, GB:N0], -1, [], "Ad")
     fill(T.NT0[:, 0:1], 66.0, [], "NTi0")
     fill(T.NT1[:, 0:1], 66.0, [], "NTi1")
     fill(T.PW[:], 0.0, [], "PW", 128)
+    if EC:
+        fill(T.EC[:], 0.0, [], "EC", 1024)
 
     names = {}
 
@@ -212,6 +212,8 @@ def rank_program(g, core, T, topo):
     for nm, f in (("B2", 2.0), ("BN", -1.0), ("BH", 1.0)):
         ts(T[nm][:], c8, PG, f, Op.is_equal, Op.mult, ["cI", "PG"], [nm], 8)
     tt(T.ZM1[:], T.tF[:], T.SAME[:], Op.mult, ["tF", "SAME"], ["ZM1"], 256)
+    for gg in range(8 * EC):
+        lin(T.EC[:, 16 * gg:2048:129], T.ZERO[:, 0:16], 0.0, T.SAME[:, 16 * gg:16 * gg + 1], ["ZERO", "SAME", "EC"], "EC%d" % gg, 16)
     lin(T.ZM0[:], T.ZM1[:], 1.0, 0.0, ["ZM1"], "ZM0")
     lin(T.ZM0[:, 0::16], T.SAME[:, 0::16], 1.0, 0.0, ["SAME"], "ZM0", 8)
     ts(T.DC[:], T.cmI[:], 15, 65.0, Op.is_equal, Op.add, ["cmI"], ["DC"])
@@ -227,6 +229,8 @@ def rank_program(g, core, T, topo):
     col("hi", 15, 1.0, "hi")
     col("nov", 11, -1.0, 1.0)
     col("nov", 15, -1.0, "nov")
+    lin(cf("xs"), cf("nov"), -1.0, 2.0, ["nov"], "xs", 1)
+    col("xb", 15, -2.0, 0.0)
     lin(cf("ct"), cf("low"), -0.5 + 2.0 ** -12, m16(12), ["low", "M16"], "ct", 1)
     col("ct", 11, 8.5, "ct")
     col("ct", 15, 9.5, "ct")
@@ -267,7 +271,6 @@ def rank_program(g, core, T, topo):
         for p in parts:
             lin(T[nm][:, p], T.SAME[:, p], -1.0, 0.0, ["SAME"], nm, 32)
     lin(T.I75[:], T.IB[:], 7.5, 0.0, ["IB"], "I75")
-    lin(T.C75[:], T.SAME[:], 0.0, 7.5, ["SAME"], "C75")
     for p in PART.values():
         lin(T.TR[:, p], T.cF[:, 0:8], 16.0, PM, ["cF", "PM"], "TR", 8)
     lin(T.WI[:], T.TR[:, 0:8], U, 0.0, ["TR"], "WI", 8)
@@ -323,8 +326,8 @@ def rank_program(g, core, T, topo):
 
     def spread(b, hs=(0, 1)):
         for h in hs:
-            for r in range(max(16 // st for lo, hi, a, st in PIECES.values() if lo // 64 == h)):
-                mm(T["zp%d%d" % (b, h)][:, :, r], T.IB[:], buf("Z", b)[:, 64 * h:64 * h + 64], True, True, ["IB", key("Z", b)], "zp%d%d" % (b, h), 64)
+            for r in range(COPIES[h]):
+                mm(T["zp%d%d" % (b, h)][:, r:64 * COPIES[h]:COPIES[h]], T.IB[:], buf("Z", b)[:, 64 * h:64 * h + 64], True, True, ["IB", key("Z", b)], "zp%d%d" % (b, h), 64)
 
     def bars(t, b, k):
         kd = key("dist", b)
@@ -334,8 +337,8 @@ def rank_program(g, core, T, topo):
 
     def maxima(t, b, p):
         lo, hi, a, st = PIECES[p]
-        kz, r = "zp%d%d" % (b, lo // 64), slice(16 * lo + a, 16 * hi, st)
-        tt(buf("M", b)[:, r], buf("D", b)[:, r], T[kz][:, lo % 64:(hi - 1) % 64 + 1, 0:16 // st], Op.max,
+        kz, r, n = "zp%d%d" % (b, lo // 64), slice(16 * lo + a, 16 * hi, st), COPIES[lo // 64]
+        tt(buf("M", b)[:, r], buf("D", b)[:, r], T[kz][:, n * (lo % 64):n * ((hi - 1) % 64 + 1):n * st // 16], Op.max,
            dk(b, lo, hi) + [kz], ["M%d%d_%d" % (b, j, i) for j in range(lo // 16, hi // 16) for i in range(a, 16, st)], 16 * (hi - lo) // st)
 
     def sums(t, b):
@@ -356,10 +359,15 @@ def rank_program(g, core, T, topo):
         mm(ch[:, 0:128], nt[:, 1:129], T.IN[:], False, True, ["IN", key("NT", b)], kc)
         gap(1)
         ts(sa, ch[:, 0:128], cf("sel"), 0.0, Op.add, Op.max, [kc, "sel"], [ks])
-        mm(ch[:, 128:256], sa, T.BLK[:], True, True, ["BLK", ks], kc)
-        gap(2)
-        tt(buf("LT", b)[:], ch[:, 128:256], T.MK[:], Op.mult, [kc, "MK"], [key("LT", b)])
-        mm(ch[:, 256:264], buf("LT", b)[:], T.BH[:], True, True, ["BH", key("LT", b)], kc, 64)
+        if EC:
+            for c in range(16):
+                mm(ch[:, 256:264], T.EC[:, 128 * c:128 * c + 128], buf("SA", b)[:, 128 * k + c:128 * k + 128:16], c == 0, c == 15, ["EC%d" % j for j in range(8)] + [ks], kc, 64)
+            gap(2)
+        else:
+            mm(ch[:, 128:256], sa, T.BLK[:], True, True, ["BLK", ks], kc)
+            gap(2)
+            tt(buf("LT", b)[:], ch[:, 128:256], T.MK[:], Op.mult, [kc, "MK"], [key("LT", b)])
+            mm(ch[:, 256:264], buf("LT", b)[:], T.BH[:], True, True, ["BH", key("LT", b)], kc, 64)
         gap(3)
         cp(vo(b), ch[:, 256:264], [kc], [key("VO", b)], 8)
         gap(4)
@@ -387,14 +395,16 @@ def rank_program(g, core, T, topo):
 
     def rows(t, b):
         kd = key("dist", b)
-        ts(buf("Rk", b)[:], T[kd][:, 256:384], cf("lo"), cf("hi"), Op.max, Op.min, [kd, "lo", "hi"], [key("Rk", b)])
+        ts(buf("Rk", b)[:, 0:128], T[kd][:, 256:384], cf("lo"), cf("hi"), Op.max, Op.min, [kd, "lo", "hi"], [key("Rk", b)])
         if t == 0:
-            lin(buf("Rl", b)[:], buf("Rk", b)[:], cf("nov"), 0.0, [key("Rk", b), "nov"], key("Rl", b))
+            lin(buf("Rl", b)[:], buf("Rk", b)[:, 0:128], cf("nov"), 0.0, [key("Rk", b), "nov"], key("Rl", b))
+        if b == 0:
+            lin(T.Rk1[:, 128:256], T.Rk0[:, 0:128], cf("xs"), cf("xb"), ["Rk0", "xs", "xb"], "Rx")
 
     def firsts(t, b, banks):
         kds = ["BD%d%d" % (b, gg) for gg in range(8)]
         for gg in range(8):
-            o, r, s1, s2 = buf("BD", b)[:, :, 16 * gg:16 * gg + 16], buf("Rk", b)[:], T.SC[:, gg:gg + 1], T.BI[:, gg:gg + 1]
+            o, r, s1, s2 = buf("BD", b)[:, :, 16 * gg:16 * gg + 16], buf("Rk", b)[:, 0:128], T.SC[:, gg:gg + 1], T.BI[:, gg:gg + 1]
             if DIAG[b][gg] == "V":
                 ts(o, r, s1, s2, Op.mult, Op.add, [key("Rk", b), "SC", "BI"], [kds[gg]], 64)
             else:
@@ -402,11 +412,11 @@ def rank_program(g, core, T, topo):
         kas = []
         for p, bks in banks:
             def part(a):
-                n, kb, lo = 16 * a + 16 if p == "l" else 128, bks[a % 2], 128 * (a // 2)
-                return n, kb, T[kb][:, lo // 8:(lo + n) // 8, :] if kb[0] == "z" else T[kb][:, lo:lo + n]
+                n, kb, lo = 16 * a + 16 if p == "l" else 128 + 128 * b, bks[a % len(bks)], 64 * len(bks) * (a // len(bks))
+                return n, kb, T[kb][:, lo:lo + n]
             for a in range(8):
                 n, kb, src = part(a)
-                mm(src, buf("BD", b)[:, a, :], buf("R" + p, b)[:, 0:n], True, True, [key("R" + p, b)] + kds, kb, max(n, 64))
+                mm(src, buf("BD", b)[:, a, :], buf("R" + p, b)[:, 0:n], True, True, [key("R" + p, b)] + ["Rx"] * (n > 128) + kds, kb, max(n, 64))
             for a in range(8):
                 n, kb, src = part(a)
                 acc, ka = buf("AC", b)[:, PART[p].start + a:PART[p].start + a + 1], "AC%s%d%d" % (p, b, a)
@@ -414,7 +424,7 @@ def rank_program(g, core, T, topo):
                 if SUMS[p + str(b)] == "VS" and a % 2 == 0:
                     op("V", lambda acc=acc, src=src: v.tensor_reduce(acc, src, AxisListType.X, Op.max), [kb], [ka], cost=n)
                 else:
-                    ac(T.junk[:, 128 * (a % 4):128 * (a % 4) + n], src, AF.Relu, [kb, "WI"], [ka, "junk%d" % (a % 4)], n + 24, bias=T.WI[:, a:a + 1], accum_out=acc)
+                    ac(T.junk[:, 256 * (a % 4):256 * (a % 4) + n], src, AF.Relu, [kb, "WI"], [ka, "junk%d" % (a % 4)], n + 24, bias=T.WI[:, a:a + 1], accum_out=acc)
         n = 8 * len(banks)
         ff, kf = buf("FF", b)[:, 0:n], key("FF", b)
         tt(ff, buf("VF", b)[:, 0:n], buf("AC", b)[:, 0:n], Op.subtract, [key("VF" + p, b) for p, _ in banks] + kas, [kf], 16)
@@ -422,21 +432,14 @@ def rank_program(g, core, T, topo):
         cp(buf("OF", b)[:, 0:n], ff, [kf], [key("OF", b)], 8)
 
     def flip(t, b):
-        o, kd, f = buf("dist", b)[:, 128:256], key("dist", b), buf("F", t)
+        o, kd = buf("dist", b)[:, 128:256], key("dist", b)
         mm(o, T.WS[:], buf("GT", b)[:], True, True, ["WS", key("GT", b)], kd)
         ac(buf("SG", b)[:], o, AF.Sign, [kd, "sg"], [key("SG", b)], bias=cf("sg"))
-        win, wk = T.X[:, 0:N0 + W + K * t].indirect(buf("OF", b)[:, 0:8]), [key("OF", b), "Xd"] + (["Xown0", "Xarr0"] if t else [])
-        if b == 0:
-            cp(f[:, 0:N0 + W + K * t].indirect(T.OF0[:, 0:8]), T.SG0[:], ["OF0", "SG0"], [key("F", t)], 128 * SCATTER)
-            mm(o, T.IB[:], T.Y0[:], True, False, ["IB", "Y0"], kd)
-            mm(o, T.I75[:], T.SG0[:], False, True, ["I75", "SG0"], kd)
-            ac(T.TV0[:], o, AF.Abs, [kd, "yc"], ["TV0"], bias=cf("yc"))
-            cp(win, T.TV0[:], wk + ["TV0"], ["X"], 128 * SCATTER)
-        else:
-            lin(T.YC[:], T.Y1[:], 1.0, -135.5, ["Y1"], "YC")
-            tt(T.FG[:], f[:, GB:N0 + W + K * t].indirect(vo(1)), T.SG1[:], Op.max, [key("F", t), "VO1", "SG1"], ["FG"], 128 * GATHER)
-            tt(T.TV1[:], T.FG[:], T.YC[:], Op.mult, ["FG", "YC"], ["TV1"], 256)
-            tt(win, T.TV1[:], T.C75[:], Op.add, wk + ["TV1", "C75"], ["X"], 128 * SCATTER)
+        mm(o, T.IB[:], buf("Y", b)[:], True, False, ["IB", key("Y", b)], kd)
+        mm(o, T.I75[:], buf("SG", b)[:], False, True, ["I75", key("SG", b)], kd)
+        ac(buf("TV", b)[:], o, AF.Abs, [kd, "yc"], [key("TV", b)], bias=cf("yc"))
+        cp(T.X[:, 0:N0 + W + K * t].indirect(buf("OF", b)[:, 0:8]), buf("TV", b)[:],
+           [key("OF", b), key("TV", b), "Xd"] + (["Xown0", "Xarr0"] if t else []), ["X"], 128 * SCATTER)
 
     def new_links(b):
         c = N0 + W + 128 * hf(b)
@@ -508,7 +511,7 @@ def rank_program(g, core, T, topo):
                     elif 0 < s and not last:
                         {"y": lambda: add_y(t, nb), "z": lambda: new_z(nb), "h": lambda: half(nb), "v": lambda: numbers(t, nb, [("V", 0, VS)]),
                          "0": lambda: spread(nb, (0,)), "1": lambda: spread(nb, (1,)), "b": lambda: bars(t, nb, nk)}[what]()
-            chain["on"] = True
+            chain["on"] = not last
             if last:
                 rows(t, 0)
             sums(t, b)
@@ -518,7 +521,7 @@ def rank_program(g, core, T, topo):
             sums_m(t, b)
             if 0 < s and not last:
                 spread(nb, (0,))
-            chain["on"] = not last
+            chain["on"] = k < S - 1
             select(b, k, gap)
             if k < S - 1:
                 links(t, b, k + 1)
@@ -531,7 +534,7 @@ def rank_program(g, core, T, topo):
             lists(t, b)
             send(t, b)
         for b in range(2):
-            firsts(t, b, [("k", ["ch0", "zp11" if b else "zp01"])] + [("l", ["ch1" if b else "ch0", "zp10" if b else "zp00"])] * (1 - t))
+            firsts(t, b, [("k", ["zp10", "zp11", "zp00", "zp01"] if b else ["zp00", "zp01"])] + [("l", ["ch1", "ch0"] if b else ["ch0", "zp11"])] * (1 - t))
             if t == 0:
                 new_links(b)
             else:

import numpy as np
from concourse.bass import DstId, RemoteDMATransfer
from concourse.mybir import dt, AluOpType as Op, AxisListType, ActivationFunctionType as AF

W, K, RO, S = 1664, 256, 2, 5
GB = 128
N0 = GB + 8
AC = N0 + W + K
MAGIC = 12582912.0
U = 4096.0
VS = 16
FILL = (48, 0)
SCUT = (64, 96)
PIECES = {"A": (0, 64, 0, 4), "B": (0, 64, 1, 4), "C": (0, 64, 2, 4), "D": (0, 64, 3, 4),
          "E": (64, 96, 0, 2), "F": (64, 96, 1, 2), "G": (96, 128, 0, 2), "H": (96, 128, 1, 2)}
COPIES = (4, 8)
PLAN = ("GHzv", "1AB", "bCDE", "", "h", "F")
ENG = (2, 4)
ARR = 4 * ENG[0] + 3 * ENG[1]
DIAG = ("SVSSVSSV", "VVSVVSVV")
SUMS = {"l0": "VS", "k0": "VS", "l1": "S", "k1": "VS"}
PART = {"k": slice(0, 8), "l": slice(8, 16)}
FIX = {"V": 40, "S": 50, "P": 0, "G": 180, "Y": 100}
GATHER, SCATTER, HOP, DMA, PE = 1.56, 3.8, 160, 2500, 0.6
PASSES = 4
EC = 1

SCRATCH = {}


def declare(where, dtype, names, shape):
    for nm in names.split():
        SCRATCH[nm] = (where, shape, dtype)


declare("sbuf", "bfloat16", "X", [128, AC + 8])
declare("sbuf", "int32", "A", [128, AC])
declare("sbuf", "int32", "w0s KI", [128, 16])
declare("sbuf", "uint16", "VO OF0 OF1", [128, 16])
declare("sbuf", "bfloat16", "XA ZS0 ZS1 ZERO WR Rk0 Rk1", [128, 256])
declare("sbuf", "bfloat16", "junk", [128, 1024])
declare("sbuf", "float32", "YV AD cF", [128, 256])
declare("sbuf", "float32", "M16 TR AC0 AC1 FF0 FF1 VF0 VF1", [128, 16])
declare("sbuf", "float32", "WI CVS CVVS SC BI", [128, 8])
declare("sbuf", "float32", "KF", [128, 40])
declare("sbuf", "bfloat16", "IB IP IN ZM0 ZM1 MK DC WC WS I75 Z0 Z1 SY0 SY1 Y0 Y1 GT0 GT1 Rl0 Rl1 SG0 SG1 TV0 TV1 ZT", [128, 128])
declare("sbuf", "bfloat16", "BD0 BD1", [128, 8, 128])
declare("sbuf", "float16", "IH I4 TRI PERM BLK WB WB4 WH4 CT AH0 AH1 LT0 LT1 HH0 HH1", [128, 128])
declare("sbuf", "float32", "tF SAME PW", [128, 128])
declare("sbuf", "int32", "cI cmI cgI VAL0 VAL1", [128, 128])
declare("sbuf", "int32", "pI", [128, 1])
declare("sbuf", "bfloat16", "B2 BN", [128, 8])
declare("sbuf", "float16", "BH", [128, 8])
declare("sbuf", "bfloat16", "D0 D1 M0 M1 EC", [128, 2048])
declare("sbuf", "uint16", "AO0 AO1", [128, 128])
declare("sbuf", "bfloat16", "NT0 NT1", [128, 136])
declare("sbuf", "float16", "SA0 SA1", [128, S * 128])
BANKS = "dist0 dist1 ch0 ch1 zp00 zp01 zp10 zp11".split()
declare("psum", "float32", " ".join(BANKS), [128, 512])
SEMAPHORES = ["qV", "qP", "qS", "qG", "ldw", "ldx", "ldal", "ldas", "ldn", "arr0", "arr1", "snt", "out1", "out2", "out3", "out4", "suc0", "suc1"]


def lay_out(calls):
    n = len(calls)
    after = [[] for _ in calls]
    for i, c in enumerate(calls):
        for j in c["before"]:
            after[j].append(i)
    tail = [0.0] * n
    for i in reversed(range(n)):
        tail[i] = calls[i]["cost"] + calls[i]["lat"] + max([tail[j] for j in after[i]] + [0.0])

    def place(order, back):
        busy, end = {c["q"]: [] for c in calls}, [0.0] * n
        for i in order:
            c = calls[i]
            if back:
                t = max([end[j] + (c["lat"] if calls[j]["before"][i] else 0) for j in after[i]] + [c["lat"]])
            else:
                t = max([end[j] + (calls[j]["lat"] if w else 0) for j, w in c["before"].items()] + [0.0])
            row = busy[c["q"]]
            at = len(row)
            while at and row[at - 1][1] > t:
                at -= 1
            while at < len(row) and row[at][0] < t + c["cost"]:
                t = max(t, row[at][1])
                at += 1
            end[i] = t + c["cost"]
            row.insert(at, (t, end[i]))
        return end
    order, best = sorted(range(n), key=lambda i: (-tail[i], i)), None
    for _ in range(PASSES):
        end = place(order, False)
        span = max(end[i] + calls[i]["lat"] for i in range(n))
        if best is None or span < best[0]:
            best = (span, sorted(range(n), key=lambda i: (end[i] - calls[i]["cost"], i)))
        end = place(sorted(range(n), key=lambda i: (-end[i], -i)), True)
        order = sorted(range(n), key=lambda i: (-end[i], i))
    return best[1]


def rank_program(g, core, T, topo):
    rank = T.rank_of(core)
    if rank is None:
        return
    sem = T.sem
    eng = {"V": g.vector, "P": g.tensor, "S": g.scalar, "G": g, "Y": g.sync}
    calls, lastw, readers, chain = [], {}, {}, {"on": False, "V": None, "S": None, "P": None}

    def op(q, f, reads, writes, acc=(), cost=128, lat=HOP, tok=None):
        before = {}
        for k in reads:
            for j in lastw.get(k, []) + [j for j in readers.get(k, []) if k in BANKS and calls[j]["q"] != q]:
                before[j] = True
        for k in list(writes) + list(acc):
            for j in lastw.get(k, []):
                before[j] = before.get(j, False) or calls[j]["q"] != q or k not in acc
            for j in readers.get(k, []):
                before[j] = before.get(j, False) or calls[j]["q"] != q or calls[j]["tok"] is not None
        if q in chain and chain["on"]:
            if chain[q] is not None:
                before.setdefault(chain[q], False)
            chain[q] = len(calls)
        calls.append({"q": q, "f": f, "before": before, "cost": FIX.get(q, 0) + cost, "lat": lat, "tok": tok})
        for k in list(writes) + list(acc):
            lastw[k], readers[k] = [len(calls) - 1], []
        for k in reads:
            readers.setdefault(k, []).append(len(calls) - 1)

    def dma(q, out, in_, name, total, reads, writes, lat=DMA):
        op(q, lambda: eng[q].dma_start(out, in_).then_inc(sem[name], 16), reads, writes, ["dma" + q], cost=0, lat=lat, tok=[(name, total)])

    v, pe, act = g.vector, g.tensor, g.scalar

    def ts(out, in0, s1, s2, o0, o1, reads, writes, c=128):
        if o1 is None:
            op("V", lambda: v.tensor_scalar(out, in0, s1, None, o0), reads, writes, cost=c)
        else:
            op("V", lambda: v.tensor_scalar(out, in0, s1, s2, o0, o1), reads, writes, cost=c)

    def tt(out, a, b, o, reads, writes, c=128):
        op("V", lambda: v.tensor_tensor(out, a, b, o), reads, writes, cost=c)

    def cp(out, in_, reads, writes, c=128):
        op("V", lambda: v.tensor_copy(out, in_), reads, writes, cost=c)

    def fill(out, x, reads, k, c=8):
        op("V", lambda: v.memset(out, x), reads, [k], cost=c)

    def ac(out, in_, f, reads, writes, c=128, **kw):
        op("S", lambda: act.activation(out, in_, f, **kw), reads, writes, cost=c)

    def lin(out, in_, scale, bias, reads, k, c=128):
        ac(out, in_, AF.Copy if isinstance(bias, float) else AF.Identity, reads, [k], c, scale=scale, bias=bias)

    def mm(out, l, r, start, stop, reads, key, c=128):
        op("P", lambda: pe.matmul(out, l, r, start, stop), reads, (), (key,), cost=c * PE)

    dma("Y", T.w0s[:], T.w0[:], "ldw", 16, [], ["w0s"])
    dma("S", T.A[0::2, N0:N0 + W], T.lk[0::2, :], "ldas", 16, [], ["A0"], 2 * DMA)
    for a, st in ((1, 4), (3, 8), (7, 16)):
        dma("Y", T.A[a::st, N0:N0 + W], T.lk[a::st, :], "ldal", 48, [], ["A%d" % a], 2 * DMA)
    dma("Y", T.A[15::16, N0:N0 + W], T.nx[:], "ldn", 16, [], ["A15"], 2 * DMA)
    dma("S", T.X[:, N0:N0 + W], T.x0[:], "ldx", 16, [], ["X"], 2 * DMA)
    op("", None, ["A0", "A1", "A3", "A7", "A15"], ["A"], cost=0, lat=0, tok=[("ldas", 16), ("ldal", 48), ("ldn", 16)])

    op("G", lambda: g.iota(T.pI[:], [[0, 1]], 0, 1), [], ["pI"], cost=2)
    op("G", lambda: g.iota(T.cI[:], [[1, 128]], 0, 0), [], ["cI"], cost=256)
    op("G", lambda: g.iota(T.cF[:], [[1, 256]], 0, 0, allow_small_or_imprecise_dtypes=True), [], ["cF"], cost=512)
    fill(T.ZERO[:], 0.0, [], "ZERO", 128)

    def stripe(nm, n, x, base, again=False):
        op("G", lambda: g.affine_select(T[nm][:], T[nm][:] if again else T.ZERO[:, 0:n], [[-1, n]], Op.not_equal, x, base, 1),
           [nm] if again else ["ZERO"], [nm], cost=2 * n)
    stripe("IB", 128, 1.0, 0)
    stripe("IP", 128, 2048.0, 0)
    stripe("IN", 128, -2048.0, 0)
    stripe("WR", 256, 63.0 / 128, 0)
    stripe("WR", 256, 63.0 / 128, 128, True)
    op("G", lambda: g.iota(T.A[:, N0 + W:AC], [[0, K]], -1, 0), ["WR"], ["Af"], cost=2 * K)
    fill(T.X[:, GB:N0], 127.0, [], "Xd")
    fill(T.X[:, AC:AC + 8], 127.0, [], "Xe")
    fill(T.A[:, GB:N0], -1, [], "Ad")
    fill(T.NT0[:, 0:1], 66.0, [], "NTi0")
    fill(T.NT1[:, 0:1], 66.0, [], "NTi1")
    fill(T.PW[:], 0.0, [], "PW", 128)
    if EC:
        fill(T.EC[:], 0.0, [], "EC", 1024)

    names = {}

    def cf(n): return T.KF[:, names.setdefault(n, len(names)):names[n] + 1]
    def ci(j): return T.KI[:, j:j + 1]
    def m16(j): return T.M16[:, j:j + 1]

    def col(n, row, scale, plus):
        lin(cf(n), m16(row), scale, plus if isinstance(plus, float) else cf(plus), ["M16"] + ([] if isinstance(plus, float) else [plus]), n, 1)
    ts(ci(0), T.pI[:], 15, None, Op.bitwise_and, None, ["pI"], ["KI0"], 1)
    ts(ci(1), T.pI[:], 4, None, Op.arith_shift_right, None, ["pI"], ["KI1"], 1)
    ts(ci(4), T.pI[:], 1, None, Op.bitwise_and, None, ["pI"], ["KI4"], 1)
    cp(cf("P0"), T.pI[:], ["pI"], ["P0"], 1)
    cp(cf("PM"), ci(0), ["KI0"], ["PM"], 1)
    cp(cf("PG"), ci(1), ["KI1"], ["PG"], 1)
    ts(T.cmI[:], T.cI[:], 15, None, Op.bitwise_and, None, ["cI"], ["cmI"])
    ts(T.cgI[:], T.cI[:], 4, None, Op.arith_shift_right, None, ["cI"], ["cgI"])
    P0, PM, PG = cf("P0"), cf("PM"), cf("PG")
    c128, c8 = T.cI[:], T.cI[:, 0:8]
    ts(T.M16[:], T.cI[:, 0:16], PM, None, Op.is_equal, None, ["cI", "PM"], ["M16"], 16)
    ts(cf("low"), PM, 10.5, None, Op.is_lt, None, ["PM"], ["low"], 1)
    ts(T.tF[:], T.cmI[:], 14.5, -1.0, Op.is_lt, Op.mult, ["cmI"], ["tF"])
    ts(T.SAME[:], T.cgI[:], PG, None, Op.is_equal, None, ["cgI", "PG"], ["SAME"])
    for nm, f in (("B2", 2.0), ("BN", -1.0), ("BH", 1.0)):
        ts(T[nm][:], c8, PG, f, Op.is_equal, Op.mult, ["cI", "PG"], [nm], 8)
    tt(T.ZM1[:], T.tF[:], T.SAME[:], Op.mult, ["tF", "SAME"], ["ZM1"], 256)
    for gg in range(8 * EC):
        lin(T.EC[:, 16 * gg:2048:129], T.ZERO[:, 0:16], 0.0, T.SAME[:, 16 * gg:16 * gg + 1], ["ZERO", "SAME", "EC"], "EC%d" % gg, 16)
    lin(T.ZM0[:], T.ZM1[:], 1.0, 0.0, ["ZM1"], "ZM0")
    lin(T.ZM0[:, 0::16], T.SAME[:, 0::16], 1.0, 0.0, ["SAME"], "ZM0", 8)
    ts(T.DC[:], T.cmI[:], 15, 65.0, Op.is_equal, Op.add, ["cmI"], ["DC"])
    col("s0", 14, -1.0, 1.0)
    col("o0", 14, -1.0, 8.0)
    col("s1", 14, -2.0, 1.0)
    col("o1", 14, float(W + K), 8.0)
    col("n14", 14, -1.0, 0.0)
    col("ad", 14, 258.0, -2.0)
    col("lo", 12, 1.0, -0.5)
    col("lo", 15, 1.0, "lo")
    col("hi", 13, 1000.0, 0.5)
    col("hi", 15, 1.0, "hi")
    col("nov", 11, -1.0, 1.0)
    col("nov", 15, -1.0, "nov")
    lin(cf("xs"), cf("nov"), -1.0, 2.0, ["nov"], "xs", 1)
    col("xb", 15, -2.0, 0.0)
    lin(cf("ct"), cf("low"), -0.5 + 2.0 ** -12, m16(12), ["low", "M16"], "ct", 1)
    col("ct", 11, 8.5, "ct")
    col("ct", 15, 9.5, "ct")
    lin(cf("sc"), cf("low"), 1024 * U, 0.0, ["low"], "sc", 1)
    col("sc", 11, 256 * U, "sc")
    col("sc", 15, -256 * U, "sc")
    col("bi", 12, -11 * 512 * U, 0.0)
    col("bi", 13, -U, "bi")
    col("bi", 11, 256 * U, "bi")
    col("bi", 15, 256 * U, "bi")
    lin(cf("i4"), cf("low"), 4095.0, 1.0, ["low"], "i4", 1)
    lin(cf("h4"), cf("low"), -4096.0, 0.0, ["low"], "h4", 1)
    fill(cf("yc"), -135.5, [], "yc", 1)
    ts(ci(2), ci(0), -1, 30, Op.mult, Op.add, ["KI0"], ["KI2"], 1)
    tt(cf("g16"), P0, PM, Op.subtract, ["P0", "PM"], ["g16"], 1)
    ts(ci(3), ci(2), 15, None, Op.bitwise_and, None, ["KI2"], ["KI3"], 1)
    ts(cf("sel"), PM, 14.5, -2048.0, Op.is_lt, Op.mult, ["PM"], ["sel"], 1)
    tt(cf("perm"), ci(3), cf("g16"), Op.add, ["KI3", "g16"], ["perm"], 1)
    cp(T.BLK[:], T.SAME[:], ["SAME"], ["BLK"])
    ts(T.PERM[:], c128, cf("perm"), None, Op.is_equal, None, ["cI", "perm"], ["PERM"])
    ts(T.MK[:], T.cmI[:], PM, None, Op.is_equal, None, ["cmI", "PM"], ["MK"])
    ts(cf("tri"), m16(15), -1000.0, P0, Op.mult, Op.add, ["M16", "P0"], ["tri"], 1)
    ts(T.tF[:], c128, cf("tri"), 1024.0, Op.is_le, Op.mult, ["cI", "tri"], ["tF"])
    tt(T.TRI[:], T.tF[:], T.SAME[:], Op.mult, ["tF", "SAME"], ["TRI"], 256)
    ts(T.VO[:], T.w0s[:], 8, None, Op.add, None, ["w0s"], ["VO0", "VO1"], 16)
    for j in range(11):
        fill(T.PW[:, j::16], 2.0 ** -(j + 1), ["PW"], "PWx%d" % j)
    tt(T.WB[:], T.PW[:], T.SAME[:], Op.mult, ["PW", "SAME"] + ["PWx%d" % j for j in range(11)], ["WB"], 256)
    ts(T.WB4[:], T.WB[:], 4096.0, None, Op.mult, None, ["WB"], ["WB4"], 64)
    cp(T.IH[:], T.IB[:], ["IB"], ["IH"], 64)
    ts(T.I4[:], T.IB[:], cf("i4"), None, Op.mult, None, ["IB", "i4"], ["I4"], 64)
    ts(T.WH4[:], T.IB[:], cf("h4"), None, Op.mult, None, ["IB", "h4"], ["WH4"], 64)
    ts(T.CT[:], c128, m16(13), cf("ct"), Op.mult, Op.add, ["cI", "M16", "ct"], ["CT"])
    ts(cf("sg"), ci(4), -7.5, 8.5, Op.mult, Op.add, ["KI4"], ["sg"], 1)
    lin(T.AD[:], T.cF[:], cf("n14"), cf("ad"), ["cF", "n14", "ad"], "AD", 256)
    for nm, parts in (("WC", (slice(11, 128, 16), slice(15, 128, 16))), ("WS", (slice(0, 128, 2),))):
        lin(T[nm][:], T.SAME[:], 0.0, 0.0, ["SAME"], nm)
        for p in parts:
            lin(T[nm][:, p], T.SAME[:, p], -1.0, 0.0, ["SAME"], nm, 32)
    lin(T.I75[:], T.IB[:], 7.5, 0.0, ["IB"], "I75")
    for p in PART.values():
        lin(T.TR[:, p], T.cF[:, 0:8], 16.0, PM, ["cF", "PM"], "TR", 8)
    lin(T.WI[:], T.TR[:, 0:8], U, 0.0, ["TR"], "WI", 8)
    lin(T.CVS[:], T.WI[:], 0.0, float(GB), ["WI"], "CVS", 8)
    lin(T.CVVS[:], T.WI[:], -1.0, float(GB), ["WI"], "CVVS", 8)
    lin(T.CVVS[:, 1::2], T.WI[:, 1::2], 0.0, float(GB), ["WI"], "CVVS", 8)
    for nm, c in (("SC", "sc"), ("BI", "bi")):
        lin(T[nm][:], T.SAME[:, 0::16], cf(c), 0.0, ["SAME", c], nm, 8)

    def hf(b): return rank // 4 if b else 1 - rank // 4
    def buf(n, b): return T[n + "%d" % b]
    def key(n, b): return "%s%d" % (n, b)
    def xread(t): return ["X", "Xd"] + (["Xe", "Xown0", "Xarr0"] if t else [])
    def xwin(t): return T.X[:, GB:AC + 8] if t else T.X[:, GB:N0 + W]
    def awin(t): return T.A[:, GB:N0 + W + K * t]
    def vo(b): return T.VO[:, 8 * hf(b):8 * hf(b) + 8]
    def wb(b): return slice(128 * b, 128 * b + 128)
    def dk(b, lo, hi): return ["D%d_%d" % (b, j) for j in range(lo // 8, hi // 8)]

    def links(t, b, k):
        new = t and k
        ts(buf("AO", b)[:], awin(1 if new else 0).indirect(vo(b)), cf("s%d" % t), cf("o%d" % t), Op.mult, Op.add,
           ["A", "Ad", key("VO", b), "s%d" % t, "o%d" % t] + (["Anew0", "Anew1"] if new else []), [key("AO", b)], 128 * GATHER)

    def half(b):
        cp(buf("AH", b)[:], buf("AO", b)[:], [key("AO", b)], [key("AH", b)], 64)
        mm(buf("ch", b)[:, 0:128], T.PERM[:], buf("AH", b)[:], True, False, ["PERM", key("AH", b)], key("ch", b))

    def gather(q, t, o, lst, n, reads, writes):
        if q == "S":
            ac(o, xwin(t).indirect(lst), AF.Copy, reads + xread(t), writes, n * GATHER, bias=128.0)
        else:
            ts(o, xwin(t).indirect(lst), 128.0, None, Op.add, None, reads + xread(t), writes, n * GATHER)

    def numbers(t, b, cuts):
        for q, lo, hi in cuts:
            if hi > lo:
                gather(q, t, buf("D", b)[:, 16 * lo:16 * hi], buf("AO", b)[:, lo:hi], 16 * (hi - lo), [key("AO", b)], dk(b, lo, hi))

    def add_y(t, b):
        if "y" in "".join(PLAN):
            return tt(buf("SY", b)[:], xwin(t).indirect(vo(b)), buf("Z", b)[:], Op.add, [key("VO", b), key("Z", b)] + xread(t), [key("SY", b)], 128 * GATHER)
        gather("S", t, buf("Y", b)[:], vo(b), 128, [key("VO", b)], [key("Y", b)])

    def halve(b):
        for nm in "ZY":
            mm(buf("dist", b)[:, 128:256], T.WR[:, 0:128], buf(nm, b)[:], nm == "Z", nm == "Y", ["WR", key(nm, b)], key("dist", b))

    def new_z(b):
        if "y" in "".join(PLAN):
            return ts(buf("Z", b)[:], buf("SY", b)[:], 0.5, 63.8, Op.mult, Op.add, [key("SY", b)], [key("Z", b)], 64)
        ts(buf("Z", b)[:], buf("dist", b)[:, 128:256], MAGIC, MAGIC - 2, Op.add, Op.subtract, [key("dist", b)], [key("Z", b)])

    def spread(b, hs=(0, 1)):
        for h in hs:
            for r in range(COPIES[h]):
                mm(T["zp%d%d" % (b, h)][:, r:64 * COPIES[h]:COPIES[h]], T.IB[:], buf("Z", b)[:, 64 * h:64 * h + 64], True, True, ["IB", key("Z", b)], "zp%d%d" % (b, h), 64)

    def bars(t, b, k):
        kd = key("dist", b)
        mm(T[kd][:, 0:128], buf("Z", b)[:], buf("ZM", t)[:], True, False, [key("ZM", t), key("Z", b)], kd)
        for k2 in range(k):
            mm(T[kd][:, 0:128], buf("SA", b)[:, wb(k2)], T.TRI[:], False, False, ["TRI", "SA%d%d" % (b, k2)], kd)

    def maxima(t, b, p):
        lo, hi, a, st = PIECES[p]
        kz, r, n = "zp%d%d" % (b, lo // 64), slice(16 * lo + a, 16 * hi, st), COPIES[lo // 64]
        tt(buf("M", b)[:, r], buf("D", b)[:, r], T[kz][:, n * (lo % 64):n * ((hi - 1) % 64 + 1):n * st // 16], Op.max,
           dk(b, lo, hi) + [kz], ["M%d%d_%d" % (b, j, i) for j in range(lo // 16, hi // 16) for i in range(a, 16, st)], 16 * (hi - lo) // st)

    def sums(t, b):
        kd = key("dist", b)
        for i in range(14 + t):
            mm(T[kd][:, 14 - i:128:16], buf("D", b)[:, i::16], T.BN[:], False, False, ["BN"] + dk(b, 0, 128), kd, 64)

    def sums_m(t, b):
        kd = key("dist", b)
        order = sorted(range(14 + t), key=lambda i: i % 2)
        for i in order:
            mm(T[kd][:, 14 - i:128:16], buf("M", b)[:, i::16], T.B2[:], False, i == order[-1], ["B2"] + ["M%d%d_%d" % (b, j, i) for j in range(8)], kd, 64)

    def select(b, k, gap):
        ch, kc, nt, sa, ks = buf("ch", b), key("ch", b), buf("NT", b), buf("SA", b)[:, wb(k)], "SA%d%d" % (b, k)
        op("V", lambda: v.tensor_tensor_scan(nt[:, 1:129], buf("dist", b)[:, 0:128], T.DC[:], 66.0, Op.min, Op.max), [key("dist", b), "DC"], [key("NT", b)])
        mm(ch[:, 0:128], nt[:, 0:128], T.IP[:], False, False, ["IP", key("NTi", b), key("NT", b)], kc)
        mm(ch[:, 0:128], nt[:, 1:129], T.IN[:], False, True, ["IN", key("NT", b)], kc)
        gap(1)
        ts(sa, ch[:, 0:128], cf("sel"), 0.0, Op.add, Op.max, [kc, "sel"], [ks])
        if EC:
            for c in range(16):
                mm(ch[:, 256:264], T.EC[:, 128 * c:128 * c + 128], buf("SA", b)[:, 128 * k + c:128 * k + 128:16], c == 0, c == 15, ["EC%d" % j for j in range(8)] + [ks], kc, 64)
            gap(2)
        else:
            mm(ch[:, 128:256], sa, T.BLK[:], True, True, ["BLK", ks], kc)
            gap(2)
            tt(buf("LT", b)[:], ch[:, 128:256], T.MK[:], Op.mult, [kc, "MK"], [key("LT", b)])
            mm(ch[:, 256:264], buf("LT", b)[:], T.BH[:], True, True, ["BH", key("LT", b)], kc, 64)
        gap(3)
        cp(vo(b), ch[:, 256:264], [kc], [key("VO", b)], 8)
        gap(4)

    def lists(t, b):
        o = buf("ch", b)[:, 256:264]
        for p in "k" if t else "kl":
            tt(buf("VF", b)[:, PART[p]], o, T["CV" + SUMS[p + str(b)]][:], Op.add, [key("ch", b), "CV" + SUMS[p + str(b)]], [key("VF" + p, b)], 8)

    def bits(t, b):
        kd, sa, ks = key("dist", b), buf("SA", b)[:, wb(S - 1)], "SA%d%d" % (b, S - 1)
        mm(T[kd][:, 128:256], T.IH[:], T.CT[:], True, False, ["IH", "CT"], kd)
        mm(T[kd][:, 128:256], T.WB[:], sa, False, True, ["WB", ks], kd)
        ts(buf("HH", b)[:], T[kd][:, 128:256], MAGIC, MAGIC, Op.add, Op.subtract, [kd], [key("HH", b)])
        mm(T[kd][:, 256:384], T.I4[:], T.CT[:], True, False, ["I4", "CT"], kd)
        mm(T[kd][:, 256:384], T.WB4[:], sa, False, False, ["WB4", ks], kd)
        mm(T[kd][:, 256:384], T.WH4[:], buf("HH", b)[:], False, False, ["WH4", key("HH", b)], kd)

    def vote(t, b):
        kd = key("dist", b)
        gather("S", t, buf("Y", b)[:], vo(b), 128, [key("VO", b)], [key("Y", b)])
        lin(buf("SY", b)[:], buf("Z", b)[:], 1.0, -128.0, [key("Z", b)], key("SY", b))
        tt(buf("GT", b)[:], xwin(t).indirect(vo(b)), buf("SY", b)[:], Op.is_gt, [key("VO", b), key("SY", b)] + xread(t), [key("GT", b)], 128 * GATHER)
        mm(T[kd][:, 256:384], T.WC[:], buf("GT", b)[:], False, True, ["WC", key("GT", b)], kd)

    def rows(t, b):
        kd = key("dist", b)
        ts(buf("Rk", b)[:, 0:128], T[kd][:, 256:384], cf("lo"), cf("hi"), Op.max, Op.min, [kd, "lo", "hi"], [key("Rk", b)])
        if t == 0:
            lin(buf("Rl", b)[:], buf("Rk", b)[:, 0:128], cf("nov"), 0.0, [key("Rk", b), "nov"], key("Rl", b))
        if b == 0:
            lin(T.Rk1[:, 128:256], T.Rk0[:, 0:128], cf("xs"), cf("xb"), ["Rk0", "xs", "xb"], "Rx")

    def firsts(t, b, banks):
        kds = ["BD%d%d" % (b, gg) for gg in range(8)]
        for gg in range(8):
            o, r, s1, s2 = buf("BD", b)[:, :, 16 * gg:16 * gg + 16], buf("Rk", b)[:, 0:128], T.SC[:, gg:gg + 1], T.BI[:, gg:gg + 1]
            if DIAG[b][gg] == "V":
                ts(o, r, s1, s2, Op.mult, Op.add, [key("Rk", b), "SC", "BI"], [kds[gg]], 64)
            else:
                ac(o, r, AF.Identity, [key("Rk", b), "SC", "BI"], [kds[gg]], scale=s1, bias=s2)
        kas = []
        for p, bks in banks:
            def part(a):
                n, kb, lo = 16 * a + 16 if p == "l" else 128 + 128 * b, bks[a % len(bks)], 64 * len(bks) * (a // len(bks))
                return n, kb, T[kb][:, lo:lo + n]
            for a in range(8):
                n, kb, src = part(a)
                mm(src, buf("BD", b)[:, a, :], buf("R" + p, b)[:, 0:n], True, True, [key("R" + p, b)] + ["Rx"] * (n > 128) + kds, kb, max(n, 64))
            for a in range(8):
                n, kb, src = part(a)
                acc, ka = buf("AC", b)[:, PART[p].start + a:PART[p].start + a + 1], "AC%s%d%d" % (p, b, a)
                kas.append(ka)
                if SUMS[p + str(b)] == "VS" and a % 2 == 0:
                    op("V", lambda acc=acc, src=src: v.tensor_reduce(acc, src, AxisListType.X, Op.max), [kb], [ka], cost=n)
                else:
                    ac(T.junk[:, 256 * (a % 4):256 * (a % 4) + n], src, AF.Relu, [kb, "WI"], [ka, "junk%d" % (a % 4)], n + 24, bias=T.WI[:, a:a + 1], accum_out=acc)
        n = 8 * len(banks)
        ff, kf = buf("FF", b)[:, 0:n], key("FF", b)
        tt(ff, buf("VF", b)[:, 0:n], buf("AC", b)[:, 0:n], Op.subtract, [key("VF" + p, b) for p, _ in banks] + kas, [kf], 16)
        tt(ff, ff, T.TR[:, 0:n], Op.max, [kf, "TR"], [kf], 16)
        cp(buf("OF", b)[:, 0:n], ff, [kf], [key("OF", b)], 8)

    def flip(t, b):
        o, kd = buf("dist", b)[:, 128:256], key("dist", b)
        mm(o, T.WS[:], buf("GT", b)[:], True, True, ["WS", key("GT", b)], kd)
        ac(buf("SG", b)[:], o, AF.Sign, [kd, "sg"], [key("SG", b)], bias=cf("sg"))
        mm(o, T.IB[:], buf("Y", b)[:], True, False, ["IB", key("Y", b)], kd)
        mm(o, T.I75[:], buf("SG", b)[:], False, True, ["I75", key("SG", b)], kd)
        ac(buf("TV", b)[:], o, AF.Abs, [kd, "yc"], [key("TV", b)], bias=cf("yc"))
        cp(T.X[:, 0:N0 + W + K * t].indirect(buf("OF", b)[:, 0:8]), buf("TV", b)[:],
           [key("OF", b), key("TV", b), "Xd"] + (["Xown0", "Xarr0"] if t else []), ["X"], 128 * SCATTER)

    def new_links(b):
        c = N0 + W + 128 * hf(b)
        tt(buf("VAL", b)[:], awin(0).indirect(vo(b)), T.AD[:, wb(hf(b))], Op.max, ["A", "Ad", key("VO", b), "AD"], [key("VAL", b)], 128 * GATHER)
        dma("Y", T.A[15::16, c:c + 128], buf("VAL", b)[15::16, :], key("suc", b), 16, [key("VAL", b), "Af"], [key("Anew", b)])
        cp(T.A[:, 0:N0 + W].indirect(buf("OF", b)[:, 8:16]), buf("VAL", b)[:], [key("OF", b), key("VAL", b), "Ad"], ["A"], 128 * SCATTER)

    def send(t, b):
        zs, o, h, kz = T["ZS%d" % t], buf("ch", b), hf(b), "ZS%d%d" % (t, b)
        for j in range(4):
            d = (4 * h + j - rank) % 8
            rot = T.WR[:, 128 - 16 * d:256 - 16 * d]
            mm(o[:, 384 + 32 * j:416 + 32 * j], rot, buf("Z", b)[:, 32 * j:32 * j + 32], True, False, ["WR", key("Z", b)], key("ch", b), 64)
            mm(o[:, 384 + 32 * j:416 + 32 * j], rot, buf("Y", b)[:, 32 * j:32 * j + 32], False, True, ["WR", key("Y", b)], key("ch", b), 64)
        c0 = N0 + W + 32 * rank
        land = T.XA[:, 32 * rank:32 * rank + 32] if t else T.X[:, c0:c0 + 32]
        if b:
            ts(zs[:, wb(h)], o[:, 384:512], MAGIC, MAGIC + 126, Op.add, Op.subtract, [key("ch", b)], [kz])
        else:
            lin(T.ZT[:], o[:, 384:512], 1.0, 2.0, [key("ch", b)], "ZT")
            lin(zs[:, wb(h)], T.ZT[:], 1.0, -128.0, ["ZT"], kz)
        trs, used = [], set()
        for q in range(4 * h, 4 * h + 4):
            if q == rank:
                continue
            dst = T.cores[q]
            es = [x for x in topo.engines(core, dst) if x not in used]
            es = es[-ENG[b]:] if dst in topo.cores_of(core) else es[:ENG[b]]
            used.update(es)
            rid, pid = topo.addr(dst, core)
            trs.append(RemoteDMATransfer(dst_ids=[DstId(rid=rid, pnc=pid)], dma_engine_mask=sum(1 << e for e in es), remote_sem=sem["arr%d" % t],
                                         src=zs[:, 32 * q:32 * q + 32], dst=land))
        op("G", lambda: g.remote_dma_fused(trs, local_sem=sem["snt"]), [kz], ["sent%d%d" % (t, b)], cost=200, lat=1.6 * DMA, tok=[])
        if b:
            lin(land, zs[:, 32 * rank:32 * rank + 32], 1.0, 0.0, [kz], "Xown%d" % t, 32)
            op("", None, ["sent%d0" % t, "sent%d1" % t], ["Xarr%d" % t], cost=0, lat=0, tok=[("arr%d" % t, ARR)])

    def final_nodes(b):
        mm(buf("ch", b)[:, 128:256], T.BLK[:], buf("SA", b)[:, wb(S - 1)], True, True, ["BLK", "SA%d%d" % (b, S - 1)], key("ch", b))
        lin(T.YV[:, wb(hf(b))], buf("ch", b)[:, 128:256], 1.0, -8.0, [key("ch", b)], key("YV", b))

    for t in range(RO):
        if t:
            dma("Y", T.yx[1::2, 0:W + K], T.X[1::2, N0:AC], "out4", 16, ["X", "Xown0", "Xarr0"], [])
        for b in range(2):
            links(t, b, 0)
            gather("V", t, buf("Z", b)[:], vo(b), 128, [key("VO", b)], [key("Z", b)])
            numbers(t, b, [("V", 0, FILL[b]), ("S", FILL[b], max(FILL[b], 64)), ("S", max(FILL[b], 64), 128)])
            spread(b)
            bars(t, b, 0)
            half(b)
        for p in PIECES:
            if p not in PLAN[0]:
                maxima(t, 0, p)
        for s in range(2 * S):
            k, b = s // 2, s % 2
            nb, nk = 1 - b, (s + 1) // 2
            last = s == 2 * S - 1

            def gap(j):
                if k == S - 1 and j == 2:
                    bits(t, b)
                if k == S - 1 and j == 4:
                    vote(t, b)
                for what in PLAN[j]:
                    if what in PIECES:
                        if j == 0 or not last:
                            maxima(t, nb if j else b, what)
                    elif 0 < s and not last:
                        {"y": lambda: add_y(t, nb), "z": lambda: new_z(nb), "h": lambda: half(nb), "v": lambda: numbers(t, nb, [("V", 0, VS)]),
                         "0": lambda: spread(nb, (0,)), "1": lambda: spread(nb, (1,)), "b": lambda: bars(t, nb, nk)}[what]()
            chain["on"] = not last
            if last:
                rows(t, 0)
            sums(t, b)
            if 0 < s and not last and "y" not in "".join(PLAN):
                halve(nb)
            gap(0)
            sums_m(t, b)
            if 0 < s and not last:
                spread(nb, (0,))
            chain["on"] = k < S - 1
            select(b, k, gap)
            if k < S - 1:
                links(t, b, k + 1)
                if "y" not in "".join(PLAN):
                    add_y(t, b)
                numbers(t, b, [("S", lo, hi) for lo, hi in zip((VS,) + SCUT, SCUT + (128,))])
            gap(5)
        rows(t, 1)
        for b in range(2):
            lists(t, b)
            send(t, b)
        for b in range(2):
            firsts(t, b, [("k", ["zp10", "zp11", "zp00", "zp01"] if b else ["zp00", "zp01"])] + [("l", ["ch1", "ch0"] if b else ["ch0", "zp11"])] * (1 - t))
            if t == 0:
                new_links(b)
            else:
                final_nodes(b)
            flip(t, b)
    dma("S", T.yx[0::2, 0:W + K], T.X[0::2, N0:AC], "out2", 16, ["X"], [], 2 * DMA)
    dma("Y", T.yv[:], T.YV[0::16, :], "out1", 16, ["YV0", "YV1"], [])
    dma("Y", T.yx[:, W + K:W + 2 * K], T.XA[:], "out3", 16, ["Xown1", "Xarr1"], [])

    clock = {q: {} for q in eng}
    cnt = {q: 0 for q in "VPSG"}
    snap = {}
    for i in lay_out(calls):
        c = calls[i]
        q = c["q"]
        if c["f"] is None:
            continue
        want = {}
        for j, waits in c["before"].items():
            for s, n in calls[j]["tok"] if waits else ():
                want[s] = max(want.get(s, 0), n)
        for s, n in want.items():
            if clock[q].get(s, 0) < n:
                eng[q].wait_ge(sem[s], n)
                for s2, n2 in list(snap.get((s, n), {}).items()) + [(s, n)]:
                    clock[q][s2] = max(clock[q].get(s2, 0), n2)
        ins = c["f"]()
        if c["tok"] is None:
            ins.then_inc(sem["q" + q], 1)
            cnt[q] += 1
            c["tok"] = [("q" + q, cnt[q])]
            snap[c["tok"][0]] = dict(clock[q])
    for s, n in [("q" + q, cnt[q]) for q in cnt] + [("snt", RO * ARR), ("arr0", ARR), ("arr1", ARR), ("ldal", 48)] + \
            [(s, 16) for s in ("out1", "out2", "out3", "out4", "suc0", "suc1", "ldw", "ldx", "ldas", "ldn")]:
        g.wait_ge(sem[s], n)
